import numpy as np, ml_dtypes
CORES = [2,6,10,14,18,22,26,30]
N = 8
BF = ml_dtypes.bfloat16
def gentries(a):
    return np.ascontiguousarray(a.reshape(8, 16, -1).transpose(0, 2, 1)).reshape(8, -1)
def gtable(e):
    e = np.asarray(e); return np.ascontiguousarray(e.reshape(8, -1, 16).transpose(0, 2, 1)).reshape(128, -1).astype(np.int32)
M, B, H, ST = 256, 8, 3, 3
W = M * B
def parts(rng):
    c = np.minimum((W * np.exp2(-5 * rng.random((N, 8, 1, W))) * rng.random((N, 8, 16, W))).astype(np.int64), W - 1)
    a = np.exp2(5 * rng.random((N, 8, 16, 1))); q = rng.choice(np.array([1, 1, 1, 16, 256]), (N, 8, 16, 1))
    l = np.minimum((W * rng.random((N, 8, 16, W)) ** a).astype(np.int64), W - 1) & -q
    gap = np.minimum((W * (0.1 + 0.8 * rng.random((N, 8, 1, M))) * (0.5 + rng.random((N, 8, 16, M)))).astype(np.int64), W - 1)
    return c, l, gap, rng.integers(0, B, (N, 8, M))
def pack(c, l, gap, cur):
    return {"ck": np.ascontiguousarray(c.reshape(N, 128, W)).astype(np.int32), "la": np.ascontiguousarray(l.reshape(N, 128, W)).astype(np.int32),
            "gap": np.ascontiguousarray(gap.reshape(N, 128, M)).astype(np.int32), "cu": np.stack([gtable(a) for a in cur])}
def setup_inputs(rng):
    return pack(*parts(rng))
def setup_inputs_ties(rng):
    c, l, gap, cur = parts(rng); c = c & -64; gap = gap & -64; l = l & -64
    kind = rng.integers(0, 4, (N, 8, 16, 1)); kind[:, :, :4, 0] = np.arange(4)
    few = np.take_along_axis(rng.integers(0, W, (N, 8, 16, 4)), rng.integers(0, kind + 1, (N, 8, 16, W)), 3)
    l[:, ::2] = few[:, ::2]
    gap = np.where((rng.random((N, 8, 1, M)) < 0.25) & (rng.random((N, 8, 16, M)) < 0.2), 0, gap)
    return pack(c, l, gap, cur)
def setup_inputs_alike(rng):
    c, l, gap, cur = parts(rng)
    c[:, ::2] = np.maximum(c[:, ::2, :1], 16); c[:, ::2, :, 0] = rng.integers(0, 16, (N, 4, 16))
    c[:, 1::2] = rng.choice(np.array([3, W // 3, W // 2, W - 1]), (N, 4, 16, W))
    cur[:, :, 0] = 0; gap[:, :, :, 0] = 0
    return pack(c, l, gap, cur)
def setup_inputs_ends(rng):
    c, l, gap, cur = parts(rng)
    c[:, 0:4] = rng.choice(np.array([0, 1, W - 2, W - 1]), (N, 4, 16, W))
    l[:, 2:6] = rng.choice(np.array([0, 1, W - 2, W - 1]), (N, 4, 16, W))
    gap[:, 1:7] = rng.choice(np.array([0, 1, W - 1]), (N, 6, 16, M))
    cur = rng.choice(np.array([0, B - 1]), (N, 8, M))
    return pack(c, l, gap, cur)
def setup_inputs_count(rng):
    c, l, gap, cur = parts(rng); c = np.maximum(c, 1)
    n = rng.choice(np.array([0, H - 1, H, H + 1, 16]), (N, 8, 1, M)); g = rng.permutation(8)
    n[:, g[0]] = 16; n[:, g[1]] = 0; n[:, g[2], 0, :5] = np.array([0, H - 1, H, H + 1, 16])
    cur[:, g[0], :B] = np.arange(B)
    n[0::2, g[3]] = 16; n[1::2, g[3]] = 0
    n[:, g[4]] = 16; l[:, g[4]] = l[:, g[4], :, :1].copy(); c[:, g[4], :, 0] = 0
    cur[:, g[4], 0] = 1; cur[:, g[4], 1:9] = (2 * np.arange(N)[:, None] + np.arange(8)) & (B - 1)
    gap = np.where(np.argsort(rng.random((N, 8, 16, M)), axis=2) < n, 0, W - 1)
    return pack(c, l, gap, cur)
def setup_inputs_spread(rng):
    c, l, gap, cur = parts(rng); e = np.log2(W)
    c = np.minimum((np.exp2(e * rng.random((N, 8, 1, W))) * rng.random((N, 8, 16, W))).astype(np.int64), W - 1)
    l = np.minimum(np.exp2(e * rng.random((N, 8, 16, W)) ** (2 * rng.random((N, 8, 16, 1)))).astype(np.int64), W - 1)
    gap = np.minimum((np.exp2(e * (1 - rng.random((N, 8, 1, M)) ** 3)) * rng.random((N, 8, 16, M))).astype(np.int64), W - 1)
    return pack(c, l, gap, cur)
def check_inputs(d):
    bad = []
    for k, hi in (("ck", W - 1), ("la", W - 1), ("gap", W - 1), ("cu", B - 1)):
        if np.min(d[k]) < 0 or np.max(d[k]) > hi: bad.append("range of " + k)
    return bad
def columns(t, x):
    return np.take_along_axis(t, np.swapaxes(x, 2, 3).reshape(N, 8, 1, 16 * M), 3).reshape(N, 8, 16, M, 16)
def reference(ck, la, gap, cu):
    C = ck.astype(np.int64).reshape(N, 8, 16, W); L = la.astype(np.int64).reshape(N, 8, 16, W); G = gap.astype(np.int64).reshape(N, 8, 16, M)
    cur = np.stack([gentries(a) for a in cu]).astype(np.int64); first = B * np.arange(M)
    I = np.take_along_axis(C, (first + cur)[:, :, None, :], 3); T = I + G
    for step in range(ST):
        A = columns(L, I); top = np.max(A, axis=4, keepdims=True)
        s = np.max(np.where(A < top, A, 0), axis=4)
        I = np.maximum(I, np.max(columns(C, s), axis=4))
        out = np.add.reduce((I >= T).astype(np.int64), axis=2) >= H
        hit = (np.arange(B) == cur[..., None]) & out[..., None]
        C = np.where(hit[:, :, None], I[..., None], C.reshape(N, 8, 16, M, B)).reshape(N, 8, 16, W)
        cur = np.where(out, (cur + 1) & (B - 1), cur)
        new = np.take_along_axis(C, (first + cur)[:, :, None, :], 3)
        T = np.where(out[:, :, None], new + G, T); I = np.where(out[:, :, None], new, I)
        I, T, G, cur = np.roll(I, 1, axis=0), np.roll(T, 1, axis=0), np.roll(G, 1, axis=0), np.roll(cur, 1, axis=0)
    return {"yi": I.reshape(N, 128, M).astype(np.float32), "yc": np.stack([gtable(a) for a in cur]).astype(np.float32)}

@@ -1,0 +1,407 @@
+from concourse.mybir import dt, AluOpType, ActivationFunctionType
+
+NQ, CH, ST, W = 4, 64, 3, 2048
+CW = CH * 16
+NC = NQ * CH
+KB = 4608.0
+
+SCRATCH = {
+    "Lt": ("sbuf", [128, W], "int32"),
+    "Cx": ("sbuf", [128, W + NC], "int32"),
+    "gapi": ("sbuf", [128, NC], "int32"),
+    "cui": ("sbuf", [128, 16], "int32"),
+    "ones": ("sbuf", [128, CW], "float32"),
+    "tE": ("sbuf", [128, CW], "float32"),
+    "tI": ("sbuf", [128, 128], "float32"),
+    "tB": ("sbuf", [128, 128], "float32"),
+    "tC": ("sbuf", [128, 128], "float32"),
+    "mask": ("sbuf", [128, CW], "float16"),
+    "Eh": ("sbuf", [128, CW], "float16"),
+    "IDh": ("sbuf", [128, 128], "float16"),
+    "NIh": ("sbuf", [128, 128], "float16"),
+    "NKh": ("sbuf", [128, 128], "float16"),
+    "BGh": ("sbuf", [128, 128], "float16"),
+    "NBh": ("sbuf", [128, 128], "float16"),
+    "LMh": ("sbuf", [128, 16 * 128], "float16"),
+    "CSh": ("sbuf", [128, 64], "float16"),
+    "j8": ("sbuf", [128, 16], "int32"),
+    "jq": ("sbuf", [128, 16], "int32"),
+    "j8a": ("sbuf", [128, 16], "int32"),
+    "i8": ("sbuf", [128, 16], "int32"),
+    "ic": ("sbuf", [128, 16], "int32"),
+    "cr": ("sbuf", [128, 64], "int32"),
+    "cm": ("sbuf", [128, 64], "int32"),
+    "ou": ("sbuf", [128, 32], "uint16"),
+    "I0": ("sbuf", [128, NC], "float16"),
+    "SL": ("sbuf", [128, NC], "uint16"),
+    "NEW": ("sbuf", [128, NC], "float16"),
+    "GE": ("sbuf", [128, NC], "float16"),
+    "REL": ("sbuf", [128, NC], "float16"),
+    "A2": ("sbuf", [128, NC], "float16"),
+    "A3": ("sbuf", [128, NC], "float16"),
+    "bls": ("sbuf", [128, 16], "float16"),
+    "lt1": ("sbuf", [128, 64], "float32"),
+    "lt2": ("sbuf", [128, 64], "float32"),
+    "YO": ("sbuf", [128, NC], "float32"),
+    "YL": ("sbuf", [128, NC], "float32"),
+    "YCO": ("sbuf", [128, 16], "float32"),
+    "YCL": ("sbuf", [128, 16], "float32"),
+    "U0": ("psum", [128, 1024], "float32"),
+    "U1": ("psum", [128, 1024], "float32"),
+    "MTp": ("psum", [128, 512], "float32"),
+    "BK": ("psum", [128, 512], "float32"),
+    "TB": ("psum", [128, 512], "float32"),
+    "AB": ("psum", [128, 512], "float32"),
+}
+for _q in range(NQ):
+    for _n in ("X", "R", "Wm", "S2", "Y", "R2"):
+        SCRATCH["%s%d" % (_n, _q)] = ("sbuf", [128, CW], "float16")
+for _q in range(2):
+    SCRATCH["MTs%d" % _q] = ("sbuf", [128, 128], "float16")
+for _t in range(ST):
+    SCRATCH["LI%d" % _t] = ("sbuf", [128, NC], "uint16")
+    SCRATCH["GP%d" % _t] = ("sbuf", [128, NC], "float16")
+    SCRATCH["E%d" % _t] = ("sbuf", [128, 80], "float32")
+    SCRATCH["RES%d" % _t] = ("sbuf", [128, 64], "float32")
+    if _t:
+        SCRATCH["IB%d" % _t] = ("sbuf", [128, 2 * NC], "float16")
+        SCRATCH["NU%d" % _t] = ("sbuf", [128, 16], "uint16")
+    if _t < ST - 1:
+        SCRATCH["OL%d" % _t] = ("sbuf", [128, NC], "uint16")
+        SCRATCH["OB%d" % _t] = ("sbuf", [128, 2 * NC], "float16")
+        SCRATCH["RU%d" % _t] = ("sbuf", [128, 48], "uint16")
+
+SEMAPHORES = ["sv", "ss", "sp", "sg", "dck", "dla", "dcu", "dgp", "loc", "ag1", "ag2", "dout", "ayc"]
+for _t in (1, 2):
+    SEMAPHORES += ["ae%d" % _t, "an%d" % _t]
+    for _q in range(NQ):
+        SEMAPHORES += ["al%d_%d" % (_t, _q), "ab%d_%d" % (_t, _q)]
+SEMAPHORES += ["ay%d" % _q for _q in range(NQ)]
+
+
+def rank_program(g, core, T, topo):
+    rank = T.rank_of(core)
+    if rank is None:
+        return
+    A, COPY = AluOpType, ActivationFunctionType.Copy
+    cores = list(T.cores)
+    n = len(cores)
+    nxt, nx2, prv, pv2 = cores[(rank + 1) % n], cores[(rank + 2) % n], cores[(rank - 1) % n], cores[(rank - 2) % n]
+    V, S, P = g.vector, g.scalar, g.tensor
+    que = {"v": V, "s": S, "p": P, "g": g, "y": g.sync}
+    own = {"v": "sv", "s": "ss", "p": "sp", "g": "sg"}
+    cnt = {"v": 0, "s": 0, "p": 0, "g": 0}
+    known, wr, rd, tot = {}, {}, {}, {"loc": 0}
+
+    def wait(q, sem, val):
+        if known.get((q, sem), 0) < val:
+            que[q].wait_ge(T.sem[sem], val)
+            known[(q, sem)] = val
+
+    def deps(q, r, w):
+        need = {}
+        mine = own.get(q)
+        for k in r:
+            if k in wr:
+                sem, val = wr[k]
+                if not (q == "p" and sem == mine):
+                    need[sem] = max(need.get(sem, 0), val)
+        for k in w:
+            toks = dict(rd.get(k, {}))
+            toks.pop(mine, None)
+            if k in wr and not (q == "p" and wr[k][0] == mine):
+                toks[wr[k][0]] = max(toks.get(wr[k][0], 0), wr[k][1])
+            for sem, val in toks.items():
+                need[sem] = max(need.get(sem, 0), val)
+        for sem, val in need.items():
+            wait(q, sem, val)
+
+    def op(q, fn, r=(), w=()):
+        deps(q, r, w)
+        fn().then_inc(T.sem[own[q]], 1)
+        cnt[q] += 1
+        for k in r:
+            rd.setdefault(k, {})[own[q]] = cnt[q]
+        for k in w:
+            wr[k] = (own[q], cnt[q])
+            rd[k] = {}
+
+    def load(q, out, in_, sem, key):
+        que[q].dma_start(out, in_).then_inc(T.sem[sem], 16)
+        wr[key] = (sem, 16)
+
+    def send(dst, out, in_, sem, r):
+        deps("g", r, ())
+        rid, pid, _ = topo.addr(dst)
+        g.remote_dma(out, in_, T.sem[sem], T.sem.loc, pid, rid, topo.mask(core, dst))
+        tot["loc"] += len(topo.engines(core, dst))
+
+    def lands(src, sem, *keys):
+        for key in keys:
+            wr[key] = (sem, len(topo.engines(src, core)))
+
+    def arr(name, k):
+        return T["%s%d" % (name, k)]
+
+    load("s", T.cui[:], T.cu[:], "dcu", "cui")
+    load("y", T.Cx[:, 0:W], T.ck[:], "dck", "C")
+    load("s", T.gapi[:], T.gap[:], "dgp", "gapi")
+    load("y", T.Lt[:], T.la[:], "dla", "Lt")
+    for t in (1, 2):
+        lands(prv, "ae%d" % t, ("E", t))
+        lands(prv, "an%d" % t, ("NU", t))
+        for q in range(NQ):
+            lands(prv, "al%d_%d" % (t, q), ("LI", t, q))
+            lands(prv, "ab%d_%d" % (t, q), ("IB", t, q))
+    lands(prv, "ag1", ("GP", 1))
+    lands(pv2, "ag2", ("GP", 2))
+
+    op("g", lambda: g.iota(T.j8[:], [[0, 16]], 0, 8), w=["j8"])
+    op("g", lambda: g.iota(T.jq[:], [[128, 16]], 0, 0), w=["jq"])
+    op("v", lambda: V.memset(T.ones[:], 1.0), w=["ones"])
+    op("g", lambda: g.affine_select(T.tI[:], T.ones[:, 0:128], [[-1, 128]], A.is_equal, 0.0, 0, 1), r=["ones"], w=["tI"])
+    op("g", lambda: g.affine_select(T.tE[:], T.ones[:], [[-1, CH], [0, 16]], A.is_equal, 0.0, 0, 1), r=["ones"], w=["tE"])
+    op("g", lambda: g.affine_select(T.tC[:], T.ones[:, 0:128], [[-16, 8], [0, 16]], A.is_ge, 0.0, 0, 1), r=["ones"], w=["tC"])
+    op("g", lambda: g.affine_select(T.tB[:], T.tC[:], [[16, 8], [0, 16]], A.is_ge, 0.0, 15, -1), r=["tC"], w=["tB"])
+    op("v", lambda: V.memset(T.mask[:], 1.0), w=["mask"])
+    op("v", lambda: V.memset(T.mask[:, 0::16], 0.0), w=["mask"])
+    op("v", lambda: V.memset(T.CSh[:], -2.5 / 16), w=["CSh"])
+    op("v", lambda: V.tensor_scalar(T.j8a[:], T.j8[:], 127, None, A.bitwise_and), r=["j8"], w=["j8a"])
+    op("v", lambda: V.tensor_tensor(T.i8[:], T.j8a[:], T.jq[:], A.add), r=["j8a", "jq"], w=["i8"])
+    op("v", lambda: V.tensor_scalar(T.ic[:], T.i8[:], 3, None, A.logical_shift_right), r=["i8"], w=["ic"])
+    op("v", lambda: V.tensor_scalar(T.E0[:, 0:16], T.ic[:], W, None, A.add), r=["ic"], w=[("E0", 4)])
+    op("v", lambda: V.tensor_scalar(T.E1[:, 0:16], T.ic[:], W, None, A.add), r=["ic"], w=["E1d"])
+    for k in range(4):
+        op("v", lambda: V.tensor_scalar(T.cr[:, 16 * k:16 * k + 16], T.cui[:], k, None, A.add), r=["cui"], w=[("cr", k)])
+    op("v", lambda: V.tensor_scalar(T.cm[:], T.cr[:], 7, None, A.bitwise_and), r=[("cr", k) for k in range(4)], w=["cm"])
+    for k in range(4):
+        op("v", lambda: V.tensor_tensor(T.E0[:, 16 + 16 * k:32 + 16 * k], T.cm[:, 16 * k:16 * k + 16], T.i8[:], A.add),
+           r=["cm", "i8"], w=[("E0", k)])
+    op("v", lambda: V.tensor_copy(T.ou[:], T.E0[:, 16:48]), r=[("E0", 0), ("E0", 1)], w=["ou"])
+    op("v", lambda: V.tensor_copy(T.IDh[:], T.tI[:]), r=["tI"], w=["IDh"])
+    op("v", lambda: V.tensor_scalar(T.NKh[:], T.tI[:], -float(W), None, A.mult), r=["tI"], w=["NKh"])
+    op("v", lambda: V.tensor_scalar(T.NIh[:], T.tI[:], -1.0, None, A.mult), r=["tI"], w=["NIh"])
+    op("v", lambda: V.tensor_copy(T.LI0[:], T.Cx[:, 0:W].indirect(T.ou[:, 0:16])), r=["C", "ou"],
+       w=[("LI", 0, q) for q in range(NQ)])
+    op("v", lambda: V.tensor_copy(T.I0[:], T.LI0[:]), r=[("LI", 0, q) for q in range(NQ)], w=[("IB", 0, q) for q in range(NQ)])
+    op("v", lambda: V.tensor_scalar(T.Eh[:], T.tE[:], float(W), None, A.mult), r=["tE"], w=["Eh"])
+    op("v", lambda: V.tensor_copy(T.GP0[:], T.gapi[:]), r=["gapi"], w=[("GP", 0)])
+    send(nxt, T.GP1[:], T.GP0[:], "ag1", [("GP", 0)])
+    send(nx2, T.GP2[:], T.GP0[:], "ag2", [("GP", 0)])
+    op("v", lambda: V.memset(T.LMh[:], 0.0), w=["LMh"])
+    op("v", lambda: V.tensor_scalar(T.BGh[:], T.tB[:], KB, None, A.mult), r=["tB"], w=["BGh"])
+    op("v", lambda: V.tensor_scalar(T.NBh[:], T.tB[:], -KB, None, A.mult), r=["tB"], w=["NBh"])
+    for m in range(16):
+        op("v", lambda: V.tensor_copy(T.LMh[:, 128 * m + m:128 * m + 128:16], T.BGh[:, m::16]), r=["BGh", "LMh"], w=[("LM", m)])
+
+    def cols(q):
+        return slice(CH * q, CH * q + CH)
+
+    def iap(t, q):
+        return T.I0[:, cols(q)] if t == 0 else arr("IB", t)[:, 2 * CH * q:2 * CH * q + CH]
+
+    def bap(t, q):
+        return T.I0[:, cols(q)] if t == 0 else arr("IB", t)[:, 2 * CH * q + CH:2 * CH * q + 2 * CH]
+
+    def Lg(t, q):
+        op("s", lambda: S.activation(arr("X", q)[:], T.Lt[:, 0:W].indirect(arr("LI", t)[:, cols(q)]), COPY),
+           r=["Lt", ("LI", t, q)], w=[("X", q)])
+
+    def Mx(q):
+        op("v", lambda: V.tensor_tensor_scan(arr("R", q)[:], T.mask[:], arr("X", q)[:], 0.0, A.mult, A.max),
+           r=["mask", ("X", q)], w=[("R", q)])
+
+    def Px(q, h):
+        op("p", lambda: P.matmul(arr("U", q % 2)[:, 512 * h:512 * h + 512], T.NKh[:], arr("X", q)[:, 512 * h:512 * h + 512], True, False),
+           r=["NKh", ("X", q)], w=[("U", q % 2, h)])
+
+    def Pt(q):
+        op("p", lambda: P.matmul(T.MTp[0:CH, 0:128], arr("R", q)[:, 15::16], T.IDh[:], True, True),
+           r=["IDh", ("R", q)], w=["MTp"])
+
+    def Mt(q):
+        op("v", lambda: V.tensor_copy(arr("MTs", q % 2)[0:CH, :], T.MTp[0:CH, 0:128]), r=["MTp"], w=[("MTs", q % 2)])
+
+    def Pe(q, h):
+        op("p", lambda: P.matmul(arr("U", q % 2)[:, 512 * h:512 * h + 512], arr("MTs", q % 2)[0:CH, :], T.Eh[0:CH, 512 * h:512 * h + 512], False, True),
+           r=["Eh", ("MTs", q % 2)], w=[("U", q % 2, h)])
+
+    def PB(q):
+        Pe(q, 0)
+        Px(q, 1)
+        Pe(q, 1)
+
+    def Wm(q):
+        for h in range(2):
+            op("v", lambda: V.tensor_tensor(arr("Wm", q)[:, 512 * h:512 * h + 512], arr("X", q)[:, 512 * h:512 * h + 512],
+                                            arr("U", q % 2)[:, 512 * h:512 * h + 512], A.min),
+               r=[("X", q), ("U", q % 2, h)], w=[("Wm", q, h)])
+
+    def Sc(q):
+        op("v", lambda: V.tensor_tensor_scan(arr("S2", q)[:], T.mask[:], arr("Wm", q)[:], 0.0, A.mult, A.max),
+           r=["mask", ("Wm", q, 0), ("Wm", q, 1)], w=[("S2", q)])
+        op("v", lambda: V.tensor_copy(T.SL[:, cols(q)], arr("S2", q)[:, 15::16]), r=[("S2", q)], w=[("SL", q)])
+
+    def Cg(q):
+        op("s", lambda: S.activation(arr("Y", q)[:], T.Cx[:, 0:W].indirect(T.SL[:, cols(q)]), COPY),
+           r=["C", ("SL", q)], w=[("Y", q)])
+
+    def Rl(t):
+        lst = T.ou[:, 16:32] if t == 0 else arr("NU", t)[:]
+        op("s", lambda: S.activation(T.REL[:], T.Cx[:, 0:W].indirect(lst), COPY), r=["C", "ou" if t == 0 else ("NU", t)], w=["REL"])
+
+    def PTI(t):
+        for q in range(NQ):
+            op("p", lambda: P.matmul(T.AB[:, cols(q)], T.IDh[:], iap(t, q), True, True), r=["IDh", ("IB", t, q)], w=["AB"])
+        for q in range(NQ):
+            op("p", lambda: P.matmul(T.TB[:, cols(q)], T.IDh[:], bap(t, q), True, False), r=["IDh", ("IB", t, q)], w=["TB"])
+            op("p", lambda: P.matmul(T.TB[:, cols(q)], T.IDh[:], arr("GP", t)[:, cols(q)], False, True), r=[("GP", t)], w=["TB"])
+
+    def Cm(q):
+        op("v", lambda: V.tensor_tensor_scan(arr("R2", q)[:], T.mask[:], arr("Y", q)[:], 0.0, A.mult, A.max),
+           r=["mask", ("Y", q)], w=[("R2", q)])
+
+    def Ge(q):
+        op("v", lambda: V.tensor_tensor(T.NEW[:, cols(q)], arr("R2", q)[:, 15::16], T.AB[:, cols(q)], A.max),
+           r=[("R2", q), "AB"], w=[("NEW", q)])
+        op("v", lambda: V.tensor_tensor(T.GE[:, cols(q)], T.NEW[:, cols(q)], T.TB[:, cols(q)], A.is_ge),
+           r=[("NEW", q), "TB"], w=[("GE", q)])
+
+    def Pb(q):
+        for k, m in ((0, "BGh"), (1, "NBh")):
+            op("p", lambda: P.matmul(T.BK[:, CH * k:CH * k + CH], T[m][:], T.CSh[:, 0:CH], True, False), r=[m, "CSh"], w=["BK"])
+            op("p", lambda: P.matmul(T.BK[:, CH * k:CH * k + CH], T[m][:], T.GE[:, cols(q)], False, True), r=[m, ("GE", q)], w=["BK"])
+
+    def Se(t, q):
+        last = t == ST - 1
+        a1 = T.AB[:, 256:256 + CH]
+        op("v", lambda: V.tensor_tensor(a1, T.REL[:, cols(q)], T.BK[:, 0:CH], A.min), r=["REL", "BK", "AB"], w=["a1"])
+        op("v", lambda: V.tensor_tensor(T.A2[:, cols(q)], T.NEW[:, cols(q)], T.BK[:, CH:2 * CH], A.min), r=[("NEW", q), "BK"], w=[("A2", q)])
+        if last:
+            op("v", lambda: V.tensor_tensor(T.YO[:, cols(q)], T.A2[:, cols(q)], a1, A.max), r=[("A2", q), "a1", "AB"], w=[("YO", q)])
+            send(nxt, T.YL[:, cols(q)], T.YO[:, cols(q)], "ay%d" % q, [("YO", q)])
+            return
+        oi = arr("OB", t)[:, 2 * CH * q:2 * CH * q + CH]
+        ob = arr("OB", t)[:, 2 * CH * q + CH:2 * CH * q + 2 * CH]
+        op("v", lambda: V.tensor_tensor(T.A3[:, cols(q)], bap(t, q), T.BK[:, CH:2 * CH], A.min), r=[("IB", t, q), "BK"], w=[("A3", q)])
+        op("v", lambda: V.tensor_tensor(oi, T.A2[:, cols(q)], a1, A.max), r=[("A2", q), "a1", "AB"], w=[("OBi", t, q)])
+        op("v", lambda: V.tensor_tensor(ob, T.A3[:, cols(q)], a1, A.max), r=[("A3", q), "a1", "AB"], w=[("OBb", t, q)])
+        op("v", lambda: V.tensor_copy(arr("OL", t)[:, cols(q)], oi), r=[("OBi", t, q)], w=[("OL", t, q)])
+        send(nxt, arr("LI", t + 1)[:, cols(q)], arr("OL", t)[:, cols(q)], "al%d_%d" % (t + 1, q), [("OL", t, q)])
+        send(nxt, arr("IB", t + 1)[:, 2 * CH * q:2 * CH * (q + 1)], arr("OB", t)[:, 2 * CH * q:2 * CH * (q + 1)], "ab%d_%d" % (t + 1, q),
+             [("OBi", t, q), ("OBb", t, q)])
+
+    def Pl():
+        op("p", lambda: P.matmul(T.TB[:, 256:272], T.BGh[:], T.CSh[:, 0:16], True, False), r=["BGh", "CSh"], w=["TB"])
+        for m in range(16):
+            op("p", lambda: P.matmul(T.TB[:, 256:272], T.LMh[:, 128 * m:128 * m + 128], T.GE[:, m::16], False, m == 15),
+               r=["LMh", ("LM", m)] + [("GE", q) for q in range(NQ)], w=["TB"])
+
+    def Vl():
+        op("v", lambda: V.tensor_copy(T.bls[:], T.TB[:, 256:272]), r=["TB"], w=["bls"])
+
+    def Pd(t):
+        for k in range((4, 3, 1)[t]):
+            op("p", lambda: P.matmul(T.TB[:, 288 + 16 * k:304 + 16 * k], T.IDh[:], T.bls[:], True, True), r=["IDh", "bls"], w=["TB"])
+            op("p", lambda: P.matmul(T.TB[:, 384 + 16 * k:400 + 16 * k], T.NIh[:], T.bls[:], True, True), r=["NIh", "bls"], w=["TB"])
+
+    def Sl(t):
+        w = 16 * (4, 3, 1)[t]
+        e = arr("E", t)
+        src = [("E0", k) for k in range(5)] if t == 0 else [("E", t)] + (["E1d"] if t == 1 else [])
+        op("v", lambda: V.tensor_tensor(T.lt1[:, 0:w], e[:, 16:16 + w], T.TB[:, 288:288 + w], A.min), r=src + ["TB"], w=["lt1"])
+        op("v", lambda: V.tensor_tensor(T.lt2[:, 0:w], e[:, 0:w], T.TB[:, 384:384 + w], A.min), r=src + ["TB"], w=["lt2"])
+        res = arr("RES", t)
+        op("v", lambda: V.tensor_tensor(res[:, 0:w], T.lt1[:, 0:w], T.lt2[:, 0:w], A.max), r=["lt1", "lt2"], w=[("RES", t)])
+        if t == ST - 1:
+            op("v", lambda: V.tensor_tensor(T.YCO[:], res[:, 0:16], T.i8[:], A.subtract), r=[("RES", t), "i8"], w=["YCO"])
+            send(nxt, T.YCL[:], T.YCO[:], "ayc", ["YCO"])
+            return
+        op("v", lambda: V.tensor_copy(arr("RU", t)[:], res[:, 0:48]), r=[("RES", t)], w=[("RU", t)])
+        send(nxt, arr("NU", t + 1)[:], arr("RU", t)[:, 32:48], "an%d" % (t + 1), [("RU", t)])
+        if t == 0:
+            send(nxt, T.E1[:, 16:64], res[:, 16:64], "ae1", [("RES", t)])
+        else:
+            send(nxt, T.E2[:, 0:32], res[:, 16:48], "ae2", [("RES", t)])
+
+    def Scat(t):
+        op("v", lambda: V.tensor_copy(T.Cx[:, 0:W + NC].indirect(arr("RU", t)[:, 0:16]), T.NEW[:]),
+           r=[("RU", t)] + [("NEW", q) for q in range(NQ)], w=["C"])
+
+    for t in range(ST):
+        Lg(t, 0)
+        Px(0, 0)
+        Mx(0)
+        Pt(0)
+        Mt(0)
+        if t:
+            Vl()
+        PB(0)
+        if t:
+            Pd(t - 1)
+        Lg(t, 1)
+        Mx(1)
+        Px(1, 0)
+        Pt(1)
+        Wm(0)
+        Mt(1)
+        PB(1)
+        if t:
+            Sl(t - 1)
+        Sc(0)
+        if t:
+            Scat(t - 1)
+        Lg(t, 2)
+        Mx(2)
+        Px(2, 0)
+        Pt(2)
+        Wm(1)
+        Mt(2)
+        PB(2)
+        Sc(1)
+        PTI(t)
+        Lg(t, 3)
+        Mx(3)
+        Px(3, 0)
+        Pt(3)
+        Wm(2)
+        Mt(3)
+        PB(3)
+        Sc(2)
+        Cg(0)
+        Rl(t)
+        Cg(1)
+        Cm(0)
+        Ge(0)
+        Pb(0)
+        Wm(3)
+        Sc(3)
+        Cg(2)
+        Cg(3)
+        Se(t, 0)
+        Cm(1)
+        Ge(1)
+        Pb(1)
+        Cm(2)
+        Se(t, 1)
+        Ge(2)
+        Pb(2)
+        Se(t, 2)
+        Cm(3)
+        Ge(3)
+        Pb(3)
+        Se(t, 3)
+        Pl()
+    Vl()
+    Pd(ST - 1)
+    Sl(ST - 1)
+
+    for q in range(NQ):
+        wait("y", "ay%d" % q, len(topo.engines(prv, core)))
+        g.sync.dma_start(T.yi[:, cols(q)], T.YL[:, cols(q)]).then_inc(T.sem.dout, 16)
+    wait("y", "ayc", len(topo.engines(prv, core)))
+    g.sync.dma_start(T.yc[:], T.YCL[:]).then_inc(T.sem.dout, 16)
+    wait("y", "dout", 16 * (NQ + 1))
+    for q in own:
+        wait("g", own[q], cnt[q])
+    wait("g", "loc", tot["loc"])

@@ -4,25 +4,39 @@ NQ, CH, ST, W = 4, 64, 3, 2048
 CW = CH * 16
 NC = NQ * CH
 KB = 4608.0
+BIG = 4096.0
+SCHED = """
+R0 L00 M00 P0 U000 W000 L01 M01 U001 W001 S00 U010 W010 L02 M02 L03 U011 W011 U020 C00 M03 S01 W020 U021 U030 W021 m00 S02 G00
+C01 W030 U031 W031 B00 E00 C02 S03 m01 F00 G01 B01 m02 E01 G02 C03 m03 L10 F01 B02 L11 G03 E02 F02 p0 v0 B03 E03 F03 d0 M10 s0
+x0 U100 U101 M11 U111 W100 L12 W101 U110 M12 U121 W111 S10 W110 L13 C10 M13 S11 C11 U120 W120 W121 m10 S12 R1 P1 G10 U130 W130
+C12 U131 W131 B10 E10 S13 m11 C13 L20 G11 F10 B11 E11 m12 F11 G12 m13 B12 E12 L21 G13 F12 M20 B13 E13 F13 p1 v1 U200 W200 M21
+U201 W201 d1 s1 U211 U210 S20 x1 L22 M22 U220 U221 L23 W211 W210 M23 U230 U231 S21 W220 W221 C20 m20 S22 W231 W230 P2 G20 B20
+S23 C21 m21 R2 E20 G21 C22 m22 B21 E21 G22 B22 C23 m23 G23 p2 E22 e2 v2 B23 E23 d2 s2
+"""
 
 SCRATCH = {
     "Lt": ("sbuf", [128, W], "int32"),
     "Cx": ("sbuf", [128, W + NC], "int32"),
     "gapi": ("sbuf", [128, NC], "int32"),
     "cui": ("sbuf", [128, 16], "int32"),
-    "ones": ("sbuf", [128, CW], "float32"),
-    "tE": ("sbuf", [128, CW], "float32"),
+    "ones": ("sbuf", [128, 128], "float32"),
     "tI": ("sbuf", [128, 128], "float32"),
     "tB": ("sbuf", [128, 128], "float32"),
     "tC": ("sbuf", [128, 128], "float32"),
+    "tD": ("sbuf", [128, 128], "float32"),
+    "tF": ("sbuf", [128, 128], "float32"),
     "mask": ("sbuf", [128, CW], "float16"),
-    "Eh": ("sbuf", [128, CW], "float16"),
     "IDh": ("sbuf", [128, 128], "float16"),
-    "NIh": ("sbuf", [128, 128], "float16"),
     "NKh": ("sbuf", [128, 128], "float16"),
+    "PKh": ("sbuf", [128, 128], "float16"),
     "BGh": ("sbuf", [128, 128], "float16"),
     "NBh": ("sbuf", [128, 128], "float16"),
-    "LMh": ("sbuf", [128, 16 * 128], "float16"),
+    "Bh": ("sbuf", [128, 128], "float16"),
+    "Ah": ("sbuf", [128, 2 * 128], "float16"),
+    "TH": ("sbuf", [128, 2 * 128], "float32"),
+    "tj": ("sbuf", [128, 2 * 128], "int32"),
+    "tk": ("sbuf", [128, 2 * 128], "int32"),
+    "te": ("sbuf", [128, 2 * 128], "float32"),
     "CSh": ("sbuf", [128, 64], "float16"),
     "j8": ("sbuf", [128, 16], "int32"),
     "jq": ("sbuf", [128, 16], "int32"),
@@ -39,16 +53,14 @@ SCRATCH = {
     "REL": ("sbuf", [128, NC], "float16"),
     "A2": ("sbuf", [128, NC], "float16"),
     "A3": ("sbuf", [128, NC], "float16"),
-    "bls": ("sbuf", [128, 16], "float16"),
     "lt1": ("sbuf", [128, 64], "float32"),
     "lt2": ("sbuf", [128, 64], "float32"),
+    "EC": ("sbuf", [128, 32], "float32"),
     "YO": ("sbuf", [128, NC], "float32"),
     "YL": ("sbuf", [128, NC], "float32"),
-    "YCO": ("sbuf", [128, 16], "float32"),
     "YCL": ("sbuf", [128, 16], "float32"),
     "U0": ("psum", [128, 1024], "float32"),
     "U1": ("psum", [128, 1024], "float32"),
-    "MTp": ("psum", [128, 512], "float32"),
     "BK": ("psum", [128, 512], "float32"),
     "TB": ("psum", [128, 512], "float32"),
     "AB": ("psum", [128, 512], "float32"),
@@ -56,8 +68,6 @@ SCRATCH = {
 for _q in range(NQ):
     for _n in ("X", "R", "Wm", "S2", "Y", "R2"):
         SCRATCH["%s%d" % (_n, _q)] = ("sbuf", [128, CW], "float16")
-for _q in range(2):
-    SCRATCH["MTs%d" % _q] = ("sbuf", [128, 128], "float16")
 for _t in range(ST):
     SCRATCH["LI%d" % _t] = ("sbuf", [128, NC], "uint16")
     SCRATCH["GP%d" % _t] = ("sbuf", [128, NC], "float16")
@@ -71,7 +81,7 @@ for _t in range(ST):
         SCRATCH["OB%d" % _t] = ("sbuf", [128, 2 * NC], "float16")
         SCRATCH["RU%d" % _t] = ("sbuf", [128, 48], "uint16")
 
-SEMAPHORES = ["sv", "ss", "sp", "sg", "dck", "dla", "dcu", "dgp", "loc", "ag1", "ag2", "dout", "ayc"]
+SEMAPHORES = ["sv", "ss", "sp", "sg", "dck", "dla", "dcu", "dgp", "loc", "ag1", "ag2", "dout", "dyc", "ayc"]
 for _t in (1, 2):
     SEMAPHORES += ["ae%d" % _t, "an%d" % _t]
     for _q in range(NQ):
@@ -136,9 +146,8 @@ def rank_program(g, core, T, topo):
         g.remote_dma(out, in_, T.sem[sem], T.sem.loc, pid, rid, topo.mask(core, dst))
         tot["loc"] += len(topo.engines(core, dst))
 
-    def lands(src, sem, *keys):
-        for key in keys:
-            wr[key] = (sem, len(topo.engines(src, core)))
+    def lands(src, sem, key):
+        wr[key] = (sem, len(topo.engines(src, core)))
 
     def arr(name, k):
         return T["%s%d" % (name, k)]
@@ -159,10 +168,14 @@ def rank_program(g, core, T, topo):
     op("g", lambda: g.iota(T.j8[:], [[0, 16]], 0, 8), w=["j8"])
     op("g", lambda: g.iota(T.jq[:], [[128, 16]], 0, 0), w=["jq"])
     op("v", lambda: V.memset(T.ones[:], 1.0), w=["ones"])
-    op("g", lambda: g.affine_select(T.tI[:], T.ones[:, 0:128], [[-1, 128]], A.is_equal, 0.0, 0, 1), r=["ones"], w=["tI"])
-    op("g", lambda: g.affine_select(T.tE[:], T.ones[:], [[-1, CH], [0, 16]], A.is_equal, 0.0, 0, 1), r=["ones"], w=["tE"])
-    op("g", lambda: g.affine_select(T.tC[:], T.ones[:, 0:128], [[-16, 8], [0, 16]], A.is_ge, 0.0, 0, 1), r=["ones"], w=["tC"])
+    op("g", lambda: g.affine_select(T.tI[:], T.ones[:], [[-1, 128]], A.is_equal, 0.0, 0, 1), r=["ones"], w=["tI"])
+    op("g", lambda: g.affine_select(T.tC[:], T.ones[:], [[-16, 8], [0, 16]], A.is_ge, 0.0, 0, 1), r=["ones"], w=["tC"])
     op("g", lambda: g.affine_select(T.tB[:], T.tC[:], [[16, 8], [0, 16]], A.is_ge, 0.0, 15, -1), r=["tC"], w=["tB"])
+    op("g", lambda: g.iota(T.tj[:], [[0, 2], [-1, 128]], 128, 1), w=["tj"])
+    for h in range(2):
+        hs = slice(64 * h, 64 * h + 64)
+        op("g", lambda: g.affine_select(T.tD[:, hs], T.ones[:, hs], [[0, 4], [-16, 16]], A.is_ge, 0.0, 128 * h, 1), r=["ones"], w=[("tD", h)])
+        op("g", lambda: g.affine_select(T.tF[:, hs], T.tD[:, hs], [[0, 4], [16, 16]], A.is_ge, 0.0, 15 - 128 * h, -1), r=[("tD", h)], w=[("tF", h)])
     op("v", lambda: V.memset(T.mask[:], 1.0), w=["mask"])
     op("v", lambda: V.memset(T.mask[:, 0::16], 0.0), w=["mask"])
     op("v", lambda: V.memset(T.CSh[:], -2.5 / 16), w=["CSh"])
@@ -171,6 +184,11 @@ def rank_program(g, core, T, topo):
     op("v", lambda: V.tensor_scalar(T.ic[:], T.i8[:], 3, None, A.logical_shift_right), r=["i8"], w=["ic"])
     op("v", lambda: V.tensor_scalar(T.E0[:, 0:16], T.ic[:], W, None, A.add), r=["ic"], w=[("E0", 4)])
     op("v", lambda: V.tensor_scalar(T.E1[:, 0:16], T.ic[:], W, None, A.add), r=["ic"], w=["E1d"])
+    op("v", lambda: V.tensor_copy(T.IDh[:], T.tI[:]), r=["tI"], w=["IDh"])
+    op("v", lambda: V.tensor_scalar(T.NKh[:], T.tI[:], -float(W), None, A.mult), r=["tI"], w=["NKh"])
+    op("v", lambda: V.tensor_scalar(T.PKh[:], T.tI[:], float(W), None, A.mult), r=["tI"], w=["PKh"])
+    op("v", lambda: V.tensor_scalar(T.BGh[:], T.tB[:], KB, None, A.mult), r=["tB"], w=["BGh"])
+    op("v", lambda: V.tensor_scalar(T.NBh[:], T.tB[:], -KB, None, A.mult), r=["tB"], w=["NBh"])
     for k in range(4):
         op("v", lambda: V.tensor_scalar(T.cr[:, 16 * k:16 * k + 16], T.cui[:], k, None, A.add), r=["cui"], w=[("cr", k)])
     op("v", lambda: V.tensor_scalar(T.cm[:], T.cr[:], 7, None, A.bitwise_and), r=[("cr", k) for k in range(4)], w=["cm"])
@@ -178,21 +196,16 @@ def rank_program(g, core, T, topo):
         op("v", lambda: V.tensor_tensor(T.E0[:, 16 + 16 * k:32 + 16 * k], T.cm[:, 16 * k:16 * k + 16], T.i8[:], A.add),
            r=["cm", "i8"], w=[("E0", k)])
     op("v", lambda: V.tensor_copy(T.ou[:], T.E0[:, 16:48]), r=[("E0", 0), ("E0", 1)], w=["ou"])
-    op("v", lambda: V.tensor_copy(T.IDh[:], T.tI[:]), r=["tI"], w=["IDh"])
-    op("v", lambda: V.tensor_scalar(T.NKh[:], T.tI[:], -float(W), None, A.mult), r=["tI"], w=["NKh"])
-    op("v", lambda: V.tensor_scalar(T.NIh[:], T.tI[:], -1.0, None, A.mult), r=["tI"], w=["NIh"])
     op("v", lambda: V.tensor_copy(T.LI0[:], T.Cx[:, 0:W].indirect(T.ou[:, 0:16])), r=["C", "ou"],
        w=[("LI", 0, q) for q in range(NQ)])
     op("v", lambda: V.tensor_copy(T.I0[:], T.LI0[:]), r=[("LI", 0, q) for q in range(NQ)], w=[("IB", 0, q) for q in range(NQ)])
-    op("v", lambda: V.tensor_scalar(T.Eh[:], T.tE[:], float(W), None, A.mult), r=["tE"], w=["Eh"])
     op("v", lambda: V.tensor_copy(T.GP0[:], T.gapi[:]), r=["gapi"], w=[("GP", 0)])
     send(nxt, T.GP1[:], T.GP0[:], "ag1", [("GP", 0)])
     send(nx2, T.GP2[:], T.GP0[:], "ag2", [("GP", 0)])
-    op("v", lambda: V.memset(T.LMh[:], 0.0), w=["LMh"])
-    op("v", lambda: V.tensor_scalar(T.BGh[:], T.tB[:], KB, None, A.mult), r=["tB"], w=["BGh"])
-    op("v", lambda: V.tensor_scalar(T.NBh[:], T.tB[:], -KB, None, A.mult), r=["tB"], w=["NBh"])
-    for m in range(16):
-        op("v", lambda: V.tensor_copy(T.LMh[:, 128 * m + m:128 * m + 128:16], T.BGh[:, m::16]), r=["BGh", "LMh"], w=[("LM", m)])
+    op("v", lambda: V.tensor_scalar(T.tk[:], T.tj[:], 15, None, A.bitwise_and), r=["tj"], w=["tk"])
+    op("v", lambda: V.tensor_scalar(T.te[:], T.tk[:], 0, None, A.is_equal), r=["tk"], w=["te"])
+    op("v", lambda: V.tensor_scalar(T.TH[:], T.te[:], -1048576.0, 1048576.0 + 2.5 * KB, A.mult, A.add), r=["te"], w=["TH"])
+    op("v", lambda: V.tensor_scalar(T.Bh[:], T.tF[:], BIG, None, A.mult), r=[("tF", 0), ("tF", 1)], w=["Bh"])
 
     def cols(q):
         return slice(CH * q, CH * q + CH)
@@ -207,42 +220,27 @@ def rank_program(g, core, T, topo):
         op("s", lambda: S.activation(arr("X", q)[:], T.Lt[:, 0:W].indirect(arr("LI", t)[:, cols(q)]), COPY),
            r=["Lt", ("LI", t, q)], w=[("X", q)])
 
-    def Mx(q):
+    def Mx(t, q):
         op("v", lambda: V.tensor_tensor_scan(arr("R", q)[:], T.mask[:], arr("X", q)[:], 0.0, A.mult, A.max),
            r=["mask", ("X", q)], w=[("R", q)])
 
-    def Px(q, h):
-        op("p", lambda: P.matmul(arr("U", q % 2)[:, 512 * h:512 * h + 512], T.NKh[:], arr("X", q)[:, 512 * h:512 * h + 512], True, False),
-           r=["NKh", ("X", q)], w=[("U", q % 2, h)])
+    def Ug(t, q, b):
+        for k in range(8 * b, 8 * b + 8):
+            o, key = arr("U", q % 2)[:, CH * k:CH * k + CH], ("U", q % 2, b)
+            op("p", lambda: P.matmul(o, T.NKh[:], arr("X", q)[:, k::16], True, False), r=["NKh", ("X", q)], w=[key])
+            op("p", lambda: P.matmul(o, T.PKh[:], arr("R", q)[:, 15::16], False, True), r=["PKh", ("R", q)], w=[key])
 
-    def Pt(q):
-        op("p", lambda: P.matmul(T.MTp[0:CH, 0:128], arr("R", q)[:, 15::16], T.IDh[:], True, True),
-           r=["IDh", ("R", q)], w=["MTp"])
+    def Wm(t, q, b):
+        for k in range(8 * b, 8 * b + 8):
+            op("v", lambda: V.tensor_tensor(arr("Wm", q)[:, k::16], arr("X", q)[:, k::16], arr("U", q % 2)[:, CH * k:CH * k + CH], A.min),
+               r=[("X", q), ("U", q % 2, b)], w=[("Wm", q, k)])
 
-    def Mt(q):
-        op("v", lambda: V.tensor_copy(arr("MTs", q % 2)[0:CH, :], T.MTp[0:CH, 0:128]), r=["MTp"], w=[("MTs", q % 2)])
-
-    def Pe(q, h):
-        op("p", lambda: P.matmul(arr("U", q % 2)[:, 512 * h:512 * h + 512], arr("MTs", q % 2)[0:CH, :], T.Eh[0:CH, 512 * h:512 * h + 512], False, True),
-           r=["Eh", ("MTs", q % 2)], w=[("U", q % 2, h)])
-
-    def PB(q):
-        Pe(q, 0)
-        Px(q, 1)
-        Pe(q, 1)
-
-    def Wm(q):
-        for h in range(2):
-            op("v", lambda: V.tensor_tensor(arr("Wm", q)[:, 512 * h:512 * h + 512], arr("X", q)[:, 512 * h:512 * h + 512],
-                                            arr("U", q % 2)[:, 512 * h:512 * h + 512], A.min),
-               r=[("X", q), ("U", q % 2, h)], w=[("Wm", q, h)])
-
-    def Sc(q):
+    def Sc(t, q):
         op("v", lambda: V.tensor_tensor_scan(arr("S2", q)[:], T.mask[:], arr("Wm", q)[:], 0.0, A.mult, A.max),
-           r=["mask", ("Wm", q, 0), ("Wm", q, 1)], w=[("S2", q)])
+           r=["mask"] + [("Wm", q, k) for k in range(16)], w=[("S2", q)])
         op("v", lambda: V.tensor_copy(T.SL[:, cols(q)], arr("S2", q)[:, 15::16]), r=[("S2", q)], w=[("SL", q)])
 
-    def Cg(q):
+    def Cg(t, q):
         op("s", lambda: S.activation(arr("Y", q)[:], T.Cx[:, 0:W].indirect(T.SL[:, cols(q)]), COPY),
            r=["C", ("SL", q)], w=[("Y", q)])
 
@@ -257,65 +255,66 @@ def rank_program(g, core, T, topo):
             op("p", lambda: P.matmul(T.TB[:, cols(q)], T.IDh[:], bap(t, q), True, False), r=["IDh", ("IB", t, q)], w=["TB"])
             op("p", lambda: P.matmul(T.TB[:, cols(q)], T.IDh[:], arr("GP", t)[:, cols(q)], False, True), r=[("GP", t)], w=["TB"])
 
-    def Cm(q):
+    def Cm(t, q):
         op("v", lambda: V.tensor_tensor_scan(arr("R2", q)[:], T.mask[:], arr("Y", q)[:], 0.0, A.mult, A.max),
            r=["mask", ("Y", q)], w=[("R2", q)])
 
-    def Ge(q):
+    def Ge(t, q):
         op("v", lambda: V.tensor_tensor(T.NEW[:, cols(q)], arr("R2", q)[:, 15::16], T.AB[:, cols(q)], A.max),
            r=[("R2", q), "AB"], w=[("NEW", q)])
         op("v", lambda: V.tensor_tensor(T.GE[:, cols(q)], T.NEW[:, cols(q)], T.TB[:, cols(q)], A.is_ge),
            r=[("NEW", q), "TB"], w=[("GE", q)])
 
-    def Pb(q):
+    def Pb(t, q):
         for k, m in ((0, "BGh"), (1, "NBh")):
             op("p", lambda: P.matmul(T.BK[:, CH * k:CH * k + CH], T[m][:], T.CSh[:, 0:CH], True, False), r=[m, "CSh"], w=["BK"])
             op("p", lambda: P.matmul(T.BK[:, CH * k:CH * k + CH], T[m][:], T.GE[:, cols(q)], False, True), r=[m, ("GE", q)], w=["BK"])
 
     def Se(t, q):
-        last = t == ST - 1
-        a1 = T.AB[:, 256:256 + CH]
-        op("v", lambda: V.tensor_tensor(a1, T.REL[:, cols(q)], T.BK[:, 0:CH], A.min), r=["REL", "BK", "AB"], w=["a1"])
+        a1 = T.AB[:, 256 + CH * q:256 + CH * q + CH]
+        op("v", lambda: V.tensor_tensor(a1, T.REL[:, cols(q)], T.BK[:, 0:CH], A.min), r=["REL", "BK", "AB"], w=[("a1", q)])
         op("v", lambda: V.tensor_tensor(T.A2[:, cols(q)], T.NEW[:, cols(q)], T.BK[:, CH:2 * CH], A.min), r=[("NEW", q), "BK"], w=[("A2", q)])
-        if last:
-            op("v", lambda: V.tensor_tensor(T.YO[:, cols(q)], T.A2[:, cols(q)], a1, A.max), r=[("A2", q), "a1", "AB"], w=[("YO", q)])
+        if t == ST - 1:
+            op("v", lambda: V.tensor_tensor(T.YO[:, cols(q)], T.A2[:, cols(q)], a1, A.max), r=[("A2", q), ("a1", q), "AB"], w=[("YO", q)])
             send(nxt, T.YL[:, cols(q)], T.YO[:, cols(q)], "ay%d" % q, [("YO", q)])
             return
         oi = arr("OB", t)[:, 2 * CH * q:2 * CH * q + CH]
-        ob = arr("OB", t)[:, 2 * CH * q + CH:2 * CH * q + 2 * CH]
-        op("v", lambda: V.tensor_tensor(T.A3[:, cols(q)], bap(t, q), T.BK[:, CH:2 * CH], A.min), r=[("IB", t, q), "BK"], w=[("A3", q)])
-        op("v", lambda: V.tensor_tensor(oi, T.A2[:, cols(q)], a1, A.max), r=[("A2", q), "a1", "AB"], w=[("OBi", t, q)])
-        op("v", lambda: V.tensor_tensor(ob, T.A3[:, cols(q)], a1, A.max), r=[("A3", q), "a1", "AB"], w=[("OBb", t, q)])
+        op("v", lambda: V.tensor_tensor(oi, T.A2[:, cols(q)], a1, A.max), r=[("A2", q), ("a1", q), "AB"], w=[("OBi", t, q)])
         op("v", lambda: V.tensor_copy(arr("OL", t)[:, cols(q)], oi), r=[("OBi", t, q)], w=[("OL", t, q)])
         send(nxt, arr("LI", t + 1)[:, cols(q)], arr("OL", t)[:, cols(q)], "al%d_%d" % (t + 1, q), [("OL", t, q)])
+
+    def Sf(t, q):
+        a1 = T.AB[:, 256 + CH * q:256 + CH * q + CH]
+        ob = arr("OB", t)[:, 2 * CH * q + CH:2 * CH * q + 2 * CH]
+        op("v", lambda: V.tensor_tensor(T.A3[:, cols(q)], bap(t, q), T.BK[:, CH:2 * CH], A.min), r=[("IB", t, q), "BK"], w=[("A3", q)])
+        op("v", lambda: V.tensor_tensor(ob, T.A3[:, cols(q)], a1, A.max), r=[("A3", q), ("a1", q), "AB"], w=[("OBb", t, q)])
         send(nxt, arr("IB", t + 1)[:, 2 * CH * q:2 * CH * (q + 1)], arr("OB", t)[:, 2 * CH * q:2 * CH * (q + 1)], "ab%d_%d" % (t + 1, q),
              [("OBi", t, q), ("OBb", t, q)])
 
-    def Pl():
-        op("p", lambda: P.matmul(T.TB[:, 256:272], T.BGh[:], T.CSh[:, 0:16], True, False), r=["BGh", "CSh"], w=["TB"])
-        for m in range(16):
-            op("p", lambda: P.matmul(T.TB[:, 256:272], T.LMh[:, 128 * m:128 * m + 128], T.GE[:, m::16], False, m == 15),
-               r=["LMh", ("LM", m)] + [("GE", q) for q in range(NQ)], w=["TB"])
+    def Pl(t):
+        for h in range(2):
+            op("p", lambda: P.matmul(T.TB[:, 256 + 128 * h:384 + 128 * h], T.GE[:, 128 * h:128 * h + 128], T.BGh[:], True, True),
+               r=["BGh"] + [("GE", q) for q in range(NQ)], w=["TB"])
 
-    def Vl():
-        op("v", lambda: V.tensor_copy(T.bls[:], T.TB[:, 256:272]), r=["TB"], w=["bls"])
+    def Vl(t):
+        op("v", lambda: V.tensor_tensor(T.Ah[:], T.TB[:, 256:512], T.TH[:], A.is_ge), r=["TB", "TH"], w=["Ah"])
 
     def Pd(t):
-        for k in range((4, 3, 1)[t]):
-            op("p", lambda: P.matmul(T.TB[:, 288 + 16 * k:304 + 16 * k], T.IDh[:], T.bls[:], True, True), r=["IDh", "bls"], w=["TB"])
-            op("p", lambda: P.matmul(T.TB[:, 384 + 16 * k:400 + 16 * k], T.NIh[:], T.bls[:], True, True), r=["NIh", "bls"], w=["TB"])
+        w = 16 * (4, 3, 1)[t]
+        for h in range(2):
+            op("p", lambda: P.matmul(T.BK[:, 128:128 + w], T.Ah[:, 128 * h:128 * h + 128], T.Bh[:, 64 * h:64 * h + w], h == 0, h == 1),
+               r=["Ah", "Bh"], w=["BK"])
 
     def Sl(t):
         w = 16 * (4, 3, 1)[t]
-        e = arr("E", t)
-        src = [("E0", k) for k in range(5)] if t == 0 else [("E", t)] + (["E1d"] if t == 1 else [])
-        op("v", lambda: V.tensor_tensor(T.lt1[:, 0:w], e[:, 16:16 + w], T.TB[:, 288:288 + w], A.min), r=src + ["TB"], w=["lt1"])
-        op("v", lambda: V.tensor_tensor(T.lt2[:, 0:w], e[:, 0:w], T.TB[:, 384:384 + w], A.min), r=src + ["TB"], w=["lt2"])
+        e = T.EC if t == ST - 1 else arr("E", t)
+        src = [("E0", k) for k in range(5)] if t == 0 else [("E", t), "E1d"] if t == 1 else ["EC0", "EC1"]
+        op("v", lambda: V.tensor_tensor(T.lt1[:, 0:w], e[:, 16:16 + w], T.BK[:, 128:128 + w], A.min), r=src + ["BK"], w=["lt1"])
+        op("v", lambda: V.tensor_tensor(T.lt2[:, 0:w], e[:, 0:w], T.BK[:, 128:128 + w], A.subtract), r=src + ["BK"], w=["lt2"])
         res = arr("RES", t)
         op("v", lambda: V.tensor_tensor(res[:, 0:w], T.lt1[:, 0:w], T.lt2[:, 0:w], A.max), r=["lt1", "lt2"], w=[("RES", t)])
         if t == ST - 1:
-            op("v", lambda: V.tensor_tensor(T.YCO[:], res[:, 0:16], T.i8[:], A.subtract), r=[("RES", t), "i8"], w=["YCO"])
-            send(nxt, T.YCL[:], T.YCO[:], "ayc", ["YCO"])
+            send(nxt, T.YCL[:], res[:, 0:16], "ayc", [("RES", t)])
             return
         op("v", lambda: V.tensor_copy(arr("RU", t)[:], res[:, 0:48]), r=[("RES", t)], w=[("RU", t)])
         send(nxt, arr("NU", t + 1)[:], arr("RU", t)[:, 32:48], "an%d" % (t + 1), [("RU", t)])
@@ -328,80 +327,23 @@ def rank_program(g, core, T, topo):
         op("v", lambda: V.tensor_copy(T.Cx[:, 0:W + NC].indirect(arr("RU", t)[:, 0:16]), T.NEW[:]),
            r=[("RU", t)] + [("NEW", q) for q in range(NQ)], w=["C"])
 
-    for t in range(ST):
-        Lg(t, 0)
-        Px(0, 0)
-        Mx(0)
-        Pt(0)
-        Mt(0)
-        if t:
-            Vl()
-        PB(0)
-        if t:
-            Pd(t - 1)
-        Lg(t, 1)
-        Mx(1)
-        Px(1, 0)
-        Pt(1)
-        Wm(0)
-        Mt(1)
-        PB(1)
-        if t:
-            Sl(t - 1)
-        Sc(0)
-        if t:
-            Scat(t - 1)
-        Lg(t, 2)
-        Mx(2)
-        Px(2, 0)
-        Pt(2)
-        Wm(1)
-        Mt(2)
-        PB(2)
-        Sc(1)
-        PTI(t)
-        Lg(t, 3)
-        Mx(3)
-        Px(3, 0)
-        Pt(3)
-        Wm(2)
-        Mt(3)
-        PB(3)
-        Sc(2)
-        Cg(0)
-        Rl(t)
-        Cg(1)
-        Cm(0)
-        Ge(0)
-        Pb(0)
-        Wm(3)
-        Sc(3)
-        Cg(2)
-        Cg(3)
-        Se(t, 0)
-        Cm(1)
-        Ge(1)
-        Pb(1)
-        Cm(2)
-        Se(t, 1)
-        Ge(2)
-        Pb(2)
-        Se(t, 2)
-        Cm(3)
-        Ge(3)
-        Pb(3)
-        Se(t, 3)
-        Pl()
-    Vl()
-    Pd(ST - 1)
-    Sl(ST - 1)
+    def Ec(t):
+        for k in range(2):
+            op("v", lambda: V.tensor_tensor(T.EC[:, 16 * k:16 * k + 16], T.E2[:, 16 * k:16 * k + 16], T.i8[:], A.subtract),
+               r=[("E", 2), "i8"], w=["EC%d" % k])
+
+    parts = {"L": Lg, "M": Mx, "U": Ug, "W": Wm, "S": Sc, "C": Cg, "R": Rl, "P": PTI, "m": Cm, "G": Ge, "B": Pb, "E": Se, "F": Sf,
+             "p": Pl, "v": Vl, "d": Pd, "s": Sl, "x": Scat, "e": Ec}
+    for tok in SCHED.split():
+        parts[tok[0]](*[int(c) for c in tok[1:]])
 
     for q in range(NQ):
         wait("y", "ay%d" % q, len(topo.engines(prv, core)))
         g.sync.dma_start(T.yi[:, cols(q)], T.YL[:, cols(q)]).then_inc(T.sem.dout, 16)
-    wait("y", "ayc", len(topo.engines(prv, core)))
-    g.sync.dma_start(T.yc[:], T.YCL[:]).then_inc(T.sem.dout, 16)
-    wait("y", "dout", 16 * (NQ + 1))
+    wait("s", "ayc", len(topo.engines(prv, core)))
+    S.dma_start(T.yc[:], T.YCL[:]).then_inc(T.sem.dyc, 16)
+    wait("s", "dyc", 16)
+    wait("y", "dout", 16 * NQ)
     for q in own:
         wait("g", own[q], cnt[q])
     wait("g", "loc", tot["loc"])

@@ -3,15 +3,18 @@ from concourse.mybir import dt, AluOpType, ActivationFunctionType
 NQ, CH, ST, W = 4, 64, 3, 2048
 CW = CH * 16
 NC = NQ * CH
+HV, TV = 32, 16
 KB = 4608.0
 BIG = 4096.0
 SCHED = """
-R0 L00 M00 P0 U000 W000 L01 M01 U001 W001 S00 U010 W010 L02 M02 L03 U011 W011 U020 C00 M03 S01 W020 U021 U030 W021 m00 S02 G00
-C01 W030 U031 W031 B00 E00 C02 S03 m01 F00 G01 B01 m02 E01 G02 C03 m03 L10 F01 B02 L11 G03 E02 F02 p0 v0 B03 E03 F03 d0 M10 s0
-x0 U100 U101 M11 U111 W100 L12 W101 U110 M12 U121 W111 S10 W110 L13 C10 M13 S11 C11 U120 W120 W121 m10 S12 R1 P1 G10 U130 W130
-C12 U131 W131 B10 E10 S13 m11 C13 L20 G11 F10 B11 E11 m12 F11 G12 m13 B12 E12 L21 G13 F12 M20 B13 E13 F13 p1 v1 U200 W200 M21
-U201 W201 d1 s1 U211 U210 S20 x1 L22 M22 U220 U221 L23 W211 W210 M23 U230 U231 S21 W220 W221 C20 m20 S22 W231 W230 P2 G20 B20
-S23 C21 m21 R2 E20 G21 C22 m22 B21 E21 G22 B22 C23 m23 G23 p2 E22 e2 v2 B23 E23 d2 s2
+L001 P0 R0 L011 l00 M00 U000 l01 M01 W000 U001 W001 L02 M02 S00 U010 W010 k00 U011 W011 L03 M03 S01 U020 W020 k01 U021 W021 C00
+m00 U030 S02 C01 U031 G00 k02 g00 B00 W030 E00 W031 H00 m01 J00 S03 k03 C02 F00 G01 g01 m02 B01 E01 G02 H01 J01 g02 F01 C03 m03
+B02 E02 G03 H02 g03 F02 J02 p0 v0 B03 E03 F03 d0 H03 L10 K00 J03 s0 M10 U100 U101 z0 K01 y0 K03 K02 L11 x0 M11 W100 L12 W101
+U111 M12 S10 L13 W111 k10 U110 W110 M13 S11 U120 W120 k11 U121 W121 C10 m10 U130 W130 P1 G10 S12 g10 k12 C11 U131 W131 R1 B10
+E10 F10 H10 J10 C12 m11 S13 G11 k13 C13 g11 B11 E11 F11 H11 K11 J11 m12 G12 g12 m13 B12 E12 G13 H12 g13 L20 F12 B13 L21 p1 J12
+L22 M20 U200 E13 F13 K12 H13 K13 J13 v1 K10 W200 d1 s1 L23 U201 M21 U211 z1 U210 W201 y1 S20 x1 k20 C20 M22 W211 W210 M23 R2
+S21 U220 W220 k21 C21 U221 W221 m20 S22 U230 W230 U231 k22 W231 P2 G20 S23 C22 g20 B20 m21 k23 G21 E20 g21 m22 c23 G22 C23 B21
+E21 m23 g22 G23 g23 e2 B22 E22 p2 H20 v2 B23 E23 H22 H21 H23 d2 s2 z2
 """
 
 SCRATCH = {
@@ -53,7 +56,6 @@ SCRATCH = {
     "REL": ("sbuf", [128, NC], "float16"),
     "A2": ("sbuf", [128, NC], "float16"),
     "A3": ("sbuf", [128, NC], "float16"),
-    "lt1": ("sbuf", [128, 64], "float32"),
     "lt2": ("sbuf", [128, 64], "float32"),
     "EC": ("sbuf", [128, 32], "float32"),
     "YO": ("sbuf", [128, NC], "float32"),
@@ -216,37 +218,54 @@ def rank_program(g, core, T, topo):
     def bap(t, q):
         return T.I0[:, cols(q)] if t == 0 else arr("IB", t)[:, 2 * CH * q + CH:2 * CH * q + 2 * CH]
 
-    def Lg(t, q):
-        op("s", lambda: S.activation(arr("X", q)[:], T.Lt[:, 0:W].indirect(arr("LI", t)[:, cols(q)]), COPY),
-           r=["Lt", ("LI", t, q)], w=[("X", q)])
+    def a1(q):
+        return T.AB[:, 256 + CH * q:256 + CH * q + CH]
+
+    def Lg(t, q, b=0):
+        k = HV * b
+        op("s", lambda: S.activation(arr("X", q)[:, 16 * k:CW], T.Lt[:, 0:W].indirect(arr("LI", t)[:, CH * q + k:CH * q + CH]), COPY),
+           r=["Lt", ("LI", t, q)], w=[("X", q, 1)] if b else [("X", q, 0), ("X", q, 1)])
+
+    def Lv(t, q):
+        op("v", lambda: V.tensor_copy(arr("X", q)[:, 0:16 * HV], T.Lt[:, 0:W].indirect(arr("LI", t)[:, CH * q:CH * q + HV])),
+           r=["Lt", ("LI", t, q)], w=[("X", q, 0)])
 
     def Mx(t, q):
         op("v", lambda: V.tensor_tensor_scan(arr("R", q)[:], T.mask[:], arr("X", q)[:], 0.0, A.mult, A.max),
-           r=["mask", ("X", q)], w=[("R", q)])
+           r=["mask", ("X", q, 0), ("X", q, 1)], w=[("R", q)])
 
     def Ug(t, q, b):
         for k in range(8 * b, 8 * b + 8):
             o, key = arr("U", q % 2)[:, CH * k:CH * k + CH], ("U", q % 2, b)
-            op("p", lambda: P.matmul(o, T.NKh[:], arr("X", q)[:, k::16], True, False), r=["NKh", ("X", q)], w=[key])
+            op("p", lambda: P.matmul(o, T.NKh[:], arr("X", q)[:, k::16], True, False), r=["NKh", ("X", q, 0), ("X", q, 1)], w=[key])
             op("p", lambda: P.matmul(o, T.PKh[:], arr("R", q)[:, 15::16], False, True), r=["PKh", ("R", q)], w=[key])
 
     def Wm(t, q, b):
         for k in range(8 * b, 8 * b + 8):
             op("v", lambda: V.tensor_tensor(arr("Wm", q)[:, k::16], arr("X", q)[:, k::16], arr("U", q % 2)[:, CH * k:CH * k + CH], A.min),
-               r=[("X", q), ("U", q % 2, b)], w=[("Wm", q, k)])
+               r=[("X", q, 0), ("X", q, 1), ("U", q % 2, b)], w=[("Wm", q, k)])
 
     def Sc(t, q):
         op("v", lambda: V.tensor_tensor_scan(arr("S2", q)[:], T.mask[:], arr("Wm", q)[:], 0.0, A.mult, A.max),
            r=["mask"] + [("Wm", q, k) for k in range(16)], w=[("S2", q)])
+
+    def Sk(t, q):
         op("v", lambda: V.tensor_copy(T.SL[:, cols(q)], arr("S2", q)[:, 15::16]), r=[("S2", q)], w=[("SL", q)])
 
     def Cg(t, q):
-        op("s", lambda: S.activation(arr("Y", q)[:], T.Cx[:, 0:W].indirect(T.SL[:, cols(q)]), COPY),
+        k = TV if (t, q) == (ST - 1, NQ - 1) else 0
+        op("s", lambda: S.activation(arr("Y", q)[:, 16 * k:CW], T.Cx[:, 0:W].indirect(T.SL[:, CH * q + k:CH * q + CH]), COPY),
            r=["C", ("SL", q)], w=[("Y", q)])
 
+    def Cv(t, q):
+        op("v", lambda: V.tensor_copy(arr("Y", q)[:, 0:16 * TV], T.Cx[:, 0:W].indirect(T.SL[:, CH * q:CH * q + TV])),
+           r=["C", ("SL", q)], w=[("Yv", q)])
+
     def Rl(t):
-        lst = T.ou[:, 16:32] if t == 0 else arr("NU", t)[:]
-        op("s", lambda: S.activation(T.REL[:], T.Cx[:, 0:W].indirect(lst), COPY), r=["C", "ou" if t == 0 else ("NU", t)], w=["REL"])
+        if t == 0:
+            op("v", lambda: V.tensor_copy(T.REL[:], T.Cx[:, 0:W].indirect(T.ou[:, 16:32])), r=["C", "ou"], w=["REL"])
+        else:
+            op("s", lambda: S.activation(T.REL[:], T.Cx[:, 0:W].indirect(arr("NU", t)[:]), COPY), r=["C", ("NU", t)], w=["REL"])
 
     def PTI(t):
         for q in range(NQ):
@@ -257,11 +276,13 @@ def rank_program(g, core, T, topo):
 
     def Cm(t, q):
         op("v", lambda: V.tensor_tensor_scan(arr("R2", q)[:], T.mask[:], arr("Y", q)[:], 0.0, A.mult, A.max),
-           r=["mask", ("Y", q)], w=[("R2", q)])
+           r=["mask", ("Y", q), ("Yv", q)], w=[("R2", q)])
 
     def Ge(t, q):
         op("v", lambda: V.tensor_tensor(T.NEW[:, cols(q)], arr("R2", q)[:, 15::16], T.AB[:, cols(q)], A.max),
            r=[("R2", q), "AB"], w=[("NEW", q)])
+
+    def Gb(t, q):
         op("v", lambda: V.tensor_tensor(T.GE[:, cols(q)], T.NEW[:, cols(q)], T.TB[:, cols(q)], A.is_ge),
            r=[("NEW", q), "TB"], w=[("GE", q)])
 
@@ -271,23 +292,25 @@ def rank_program(g, core, T, topo):
             op("p", lambda: P.matmul(T.BK[:, CH * k:CH * k + CH], T[m][:], T.GE[:, cols(q)], False, True), r=[m, ("GE", q)], w=["BK"])
 
     def Se(t, q):
-        a1 = T.AB[:, 256 + CH * q:256 + CH * q + CH]
-        op("v", lambda: V.tensor_tensor(a1, T.REL[:, cols(q)], T.BK[:, 0:CH], A.min), r=["REL", "BK", "AB"], w=[("a1", q)])
+        op("v", lambda: V.tensor_tensor(a1(q), T.REL[:, cols(q)], T.BK[:, 0:CH], A.min), r=["REL", "BK", "AB"], w=[("a1", q)])
         op("v", lambda: V.tensor_tensor(T.A2[:, cols(q)], T.NEW[:, cols(q)], T.BK[:, CH:2 * CH], A.min), r=[("NEW", q), "BK"], w=[("A2", q)])
+
+    def Sh(t, q):
+        o = T.YO[:, cols(q)] if t == ST - 1 else arr("OB", t)[:, 2 * CH * q:2 * CH * q + CH]
+        op("v", lambda: V.tensor_tensor(o, T.A2[:, cols(q)], a1(q), A.max), r=[("A2", q), ("a1", q), "AB"], w=[("OBi", t, q)])
         if t == ST - 1:
-            op("v", lambda: V.tensor_tensor(T.YO[:, cols(q)], T.A2[:, cols(q)], a1, A.max), r=[("A2", q), ("a1", q), "AB"], w=[("YO", q)])
-            send(nxt, T.YL[:, cols(q)], T.YO[:, cols(q)], "ay%d" % q, [("YO", q)])
-            return
-        oi = arr("OB", t)[:, 2 * CH * q:2 * CH * q + CH]
-        op("v", lambda: V.tensor_tensor(oi, T.A2[:, cols(q)], a1, A.max), r=[("A2", q), ("a1", q), "AB"], w=[("OBi", t, q)])
-        op("v", lambda: V.tensor_copy(arr("OL", t)[:, cols(q)], oi), r=[("OBi", t, q)], w=[("OL", t, q)])
+            send(nxt, T.YL[:, cols(q)], T.YO[:, cols(q)], "ay%d" % q, [("OBi", t, q)])
+
+    def Sj(t, q):
+        op("v", lambda: V.tensor_copy(arr("OL", t)[:, cols(q)], arr("OB", t)[:, 2 * CH * q:2 * CH * q + CH]), r=[("OBi", t, q)], w=[("OL", t, q)])
         send(nxt, arr("LI", t + 1)[:, cols(q)], arr("OL", t)[:, cols(q)], "al%d_%d" % (t + 1, q), [("OL", t, q)])
 
     def Sf(t, q):
-        a1 = T.AB[:, 256 + CH * q:256 + CH * q + CH]
-        ob = arr("OB", t)[:, 2 * CH * q + CH:2 * CH * q + 2 * CH]
         op("v", lambda: V.tensor_tensor(T.A3[:, cols(q)], bap(t, q), T.BK[:, CH:2 * CH], A.min), r=[("IB", t, q), "BK"], w=[("A3", q)])
-        op("v", lambda: V.tensor_tensor(ob, T.A3[:, cols(q)], a1, A.max), r=[("A3", q), ("a1", q), "AB"], w=[("OBb", t, q)])
+
+    def Sb(t, q):
+        ob = arr("OB", t)[:, 2 * CH * q + CH:2 * CH * q + 2 * CH]
+        op("v", lambda: V.tensor_tensor(ob, T.A3[:, cols(q)], a1(q), A.max), r=[("A3", q), ("a1", q), "AB"], w=[("OBb", t, q)])
         send(nxt, arr("IB", t + 1)[:, 2 * CH * q:2 * CH * (q + 1)], arr("OB", t)[:, 2 * CH * q:2 * CH * (q + 1)], "ab%d_%d" % (t + 1, q),
              [("OBi", t, q), ("OBb", t, q)])
 
@@ -309,13 +332,18 @@ def rank_program(g, core, T, topo):
         w = 16 * (4, 3, 1)[t]
         e = T.EC if t == ST - 1 else arr("E", t)
         src = [("E0", k) for k in range(5)] if t == 0 else [("E", t), "E1d"] if t == 1 else ["EC0", "EC1"]
-        op("v", lambda: V.tensor_tensor(T.lt1[:, 0:w], e[:, 16:16 + w], T.BK[:, 128:128 + w], A.min), r=src + ["BK"], w=["lt1"])
+        op("v", lambda: V.tensor_tensor(T.BK[:, 192:192 + w], e[:, 16:16 + w], T.BK[:, 128:128 + w], A.min), r=src + ["BK"], w=["lt1"])
         op("v", lambda: V.tensor_tensor(T.lt2[:, 0:w], e[:, 0:w], T.BK[:, 128:128 + w], A.subtract), r=src + ["BK"], w=["lt2"])
+
+    def Sz(t):
+        w = 16 * (4, 3, 1)[t]
         res = arr("RES", t)
-        op("v", lambda: V.tensor_tensor(res[:, 0:w], T.lt1[:, 0:w], T.lt2[:, 0:w], A.max), r=["lt1", "lt2"], w=[("RES", t)])
+        op("v", lambda: V.tensor_tensor(res[:, 0:w], T.lt2[:, 0:w], T.BK[:, 192:192 + w], A.max), r=["lt1", "lt2", "BK"], w=[("RES", t)])
         if t == ST - 1:
             send(nxt, T.YCL[:], res[:, 0:16], "ayc", [("RES", t)])
-            return
+
+    def Sy(t):
+        res = arr("RES", t)
         op("v", lambda: V.tensor_copy(arr("RU", t)[:], res[:, 0:48]), r=[("RES", t)], w=[("RU", t)])
         send(nxt, arr("NU", t + 1)[:], arr("RU", t)[:, 32:48], "an%d" % (t + 1), [("RU", t)])
         if t == 0:
@@ -332,8 +360,8 @@ def rank_program(g, core, T, topo):
             op("v", lambda: V.tensor_tensor(T.EC[:, 16 * k:16 * k + 16], T.E2[:, 16 * k:16 * k + 16], T.i8[:], A.subtract),
                r=[("E", 2), "i8"], w=["EC%d" % k])
 
-    parts = {"L": Lg, "M": Mx, "U": Ug, "W": Wm, "S": Sc, "C": Cg, "R": Rl, "P": PTI, "m": Cm, "G": Ge, "B": Pb, "E": Se, "F": Sf,
-             "p": Pl, "v": Vl, "d": Pd, "s": Sl, "x": Scat, "e": Ec}
+    parts = {"L": Lg, "l": Lv, "M": Mx, "U": Ug, "W": Wm, "S": Sc, "k": Sk, "C": Cg, "c": Cv, "R": Rl, "P": PTI, "m": Cm, "G": Ge, "g": Gb,
+             "B": Pb, "E": Se, "H": Sh, "J": Sj, "F": Sf, "K": Sb, "p": Pl, "v": Vl, "d": Pd, "s": Sl, "z": Sz, "y": Sy, "x": Scat, "e": Ec}
     for tok in SCHED.split():
         parts[tok[0]](*[int(c) for c in tok[1:]])
 

from concourse.mybir import dt, AluOpType, ActivationFunctionType

NQ, CH, ST, W = 4, 64, 3, 2048
CW = CH * 16
NC = NQ * CH
HV, TV = 32, 16
KB = 4608.0
BIG = 4096.0
SCHED = """
L001 P0 R0 L011 l00 M00 U000 l01 M01 W000 U001 W001 L02 M02 S00 U010 W010 k00 U011 W011 L03 M03 S01 U020 W020 k01 U021 W021 C00
m00 U030 S02 C01 U031 G00 k02 g00 B00 W030 E00 W031 H00 m01 J00 S03 k03 C02 F00 G01 g01 m02 B01 E01 G02 H01 J01 g02 F01 C03 m03
B02 E02 G03 H02 g03 F02 J02 p0 v0 B03 E03 F03 d0 H03 L10 K00 J03 s0 M10 U100 U101 z0 K01 y0 K03 K02 L11 x0 M11 W100 L12 W101
U111 M12 S10 L13 W111 k10 U110 W110 M13 S11 U120 W120 k11 U121 W121 C10 m10 U130 W130 P1 G10 S12 g10 k12 C11 U131 W131 R1 B10
E10 F10 H10 J10 C12 m11 S13 G11 k13 C13 g11 B11 E11 F11 H11 K11 J11 m12 G12 g12 m13 B12 E12 G13 H12 g13 L20 F12 B13 L21 p1 J12
L22 M20 U200 E13 F13 K12 H13 K13 J13 v1 K10 W200 d1 s1 L23 U201 M21 U211 z1 U210 W201 y1 S20 x1 k20 C20 M22 W211 W210 M23 R2
S21 U220 W220 k21 C21 U221 W221 m20 S22 U230 W230 U231 k22 W231 P2 G20 S23 C22 g20 B20 m21 k23 G21 E20 g21 m22 c23 G22 C23 B21
E21 m23 g22 G23 g23 e2 B22 E22 p2 H20 v2 B23 E23 H22 H21 H23 d2 s2 z2
"""

SCRATCH = {
    "Lt": ("sbuf", [128, W], "int32"),
    "Cx": ("sbuf", [128, W + NC], "int32"),
    "gapi": ("sbuf", [128, NC], "int32"),
    "cui": ("sbuf", [128, 16], "int32"),
    "ones": ("sbuf", [128, 128], "float32"),
    "tI": ("sbuf", [128, 128], "float32"),
    "tB": ("sbuf", [128, 128], "float32"),
    "tC": ("sbuf", [128, 128], "float32"),
    "tD": ("sbuf", [128, 128], "float32"),
    "tF": ("sbuf", [128, 128], "float32"),
    "mask": ("sbuf", [128, CW], "float16"),
    "IDh": ("sbuf", [128, 128], "float16"),
    "NKh": ("sbuf", [128, 128], "float16"),
    "PKh": ("sbuf", [128, 128], "float16"),
    "BGh": ("sbuf", [128, 128], "float16"),
    "NBh": ("sbuf", [128, 128], "float16"),
    "Bh": ("sbuf", [128, 128], "float16"),
    "Ah": ("sbuf", [128, 2 * 128], "float16"),
    "TH": ("sbuf", [128, 2 * 128], "float32"),
    "tj": ("sbuf", [128, 2 * 128], "int32"),
    "tk": ("sbuf", [128, 2 * 128], "int32"),
    "te": ("sbuf", [128, 2 * 128], "float32"),
    "CSh": ("sbuf", [128, 64], "float16"),
    "j8": ("sbuf", [128, 16], "int32"),
    "jq": ("sbuf", [128, 16], "int32"),
    "j8a": ("sbuf", [128, 16], "int32"),
    "i8": ("sbuf", [128, 16], "int32"),
    "ic": ("sbuf", [128, 16], "int32"),
    "cr": ("sbuf", [128, 64], "int32"),
    "cm": ("sbuf", [128, 64], "int32"),
    "ou": ("sbuf", [128, 32], "uint16"),
    "I0": ("sbuf", [128, NC], "float16"),
    "SL": ("sbuf", [128, NC], "uint16"),
    "NEW": ("sbuf", [128, NC], "float16"),
    "GE": ("sbuf", [128, NC], "float16"),
    "REL": ("sbuf", [128, NC], "float16"),
    "A2": ("sbuf", [128, NC], "float16"),
    "A3": ("sbuf", [128, NC], "float16"),
    "lt2": ("sbuf", [128, 64], "float32"),
    "EC": ("sbuf", [128, 32], "float32"),
    "YO": ("sbuf", [128, NC], "float32"),
    "YL": ("sbuf", [128, NC], "float32"),
    "YCL": ("sbuf", [128, 16], "float32"),
    "U0": ("psum", [128, 1024], "float32"),
    "U1": ("psum", [128, 1024], "float32"),
    "BK": ("psum", [128, 512], "float32"),
    "TB": ("psum", [128, 512], "float32"),
    "AB": ("psum", [128, 512], "float32"),
}
for _q in range(NQ):
    for _n in ("X", "R", "Wm", "S2", "Y", "R2"):
        SCRATCH["%s%d" % (_n, _q)] = ("sbuf", [128, CW], "float16")
for _t in range(ST):
    SCRATCH["LI%d" % _t] = ("sbuf", [128, NC], "uint16")
    SCRATCH["GP%d" % _t] = ("sbuf", [128, NC], "float16")
    SCRATCH["E%d" % _t] = ("sbuf", [128, 80], "float32")
    SCRATCH["RES%d" % _t] = ("sbuf", [128, 64], "float32")
    if _t:
        SCRATCH["IB%d" % _t] = ("sbuf", [128, 2 * NC], "float16")
        SCRATCH["NU%d" % _t] = ("sbuf", [128, 16], "uint16")
    if _t < ST - 1:
        SCRATCH["OL%d" % _t] = ("sbuf", [128, NC], "uint16")
        SCRATCH["OB%d" % _t] = ("sbuf", [128, 2 * NC], "float16")
        SCRATCH["RU%d" % _t] = ("sbuf", [128, 48], "uint16")

SEMAPHORES = ["sv", "ss", "sp", "sg", "dck", "dla", "dcu", "dgp", "loc", "ag1", "ag2", "dout", "dyc", "ayc"]
for _t in (1, 2):
    SEMAPHORES += ["ae%d" % _t, "an%d" % _t]
    for _q in range(NQ):
        SEMAPHORES += ["al%d_%d" % (_t, _q), "ab%d_%d" % (_t, _q)]
SEMAPHORES += ["ay%d" % _q for _q in range(NQ)]


def rank_program(g, core, T, topo):
    rank = T.rank_of(core)
    if rank is None:
        return
    A, COPY = AluOpType, ActivationFunctionType.Copy
    cores = list(T.cores)
    n = len(cores)
    nxt, nx2, prv, pv2 = cores[(rank + 1) % n], cores[(rank + 2) % n], cores[(rank - 1) % n], cores[(rank - 2) % n]
    V, S, P = g.vector, g.scalar, g.tensor
    que = {"v": V, "s": S, "p": P, "g": g, "y": g.sync}
    own = {"v": "sv", "s": "ss", "p": "sp", "g": "sg"}
    cnt = {"v": 0, "s": 0, "p": 0, "g": 0}
    known, wr, rd, tot = {}, {}, {}, {"loc": 0}

    def wait(q, sem, val):
        if known.get((q, sem), 0) < val:
            que[q].wait_ge(T.sem[sem], val)
            known[(q, sem)] = val

    def deps(q, r, w):
        need = {}
        mine = own.get(q)
        for k in r:
            if k in wr:
                sem, val = wr[k]
                if not (q == "p" and sem == mine):
                    need[sem] = max(need.get(sem, 0), val)
        for k in w:
            toks = dict(rd.get(k, {}))
            toks.pop(mine, None)
            if k in wr and not (q == "p" and wr[k][0] == mine):
                toks[wr[k][0]] = max(toks.get(wr[k][0], 0), wr[k][1])
            for sem, val in toks.items():
                need[sem] = max(need.get(sem, 0), val)
        for sem, val in need.items():
            wait(q, sem, val)

    def op(q, fn, r=(), w=()):
        deps(q, r, w)
        fn().then_inc(T.sem[own[q]], 1)
        cnt[q] += 1
        for k in r:
            rd.setdefault(k, {})[own[q]] = cnt[q]
        for k in w:
            wr[k] = (own[q], cnt[q])
            rd[k] = {}

    def load(q, out, in_, sem, key):
        que[q].dma_start(out, in_).then_inc(T.sem[sem], 16)
        wr[key] = (sem, 16)

    def send(dst, out, in_, sem, r):
        deps("g", r, ())
        rid, pid, _ = topo.addr(dst)
        g.remote_dma(out, in_, T.sem[sem], T.sem.loc, pid, rid, topo.mask(core, dst))
        tot["loc"] += len(topo.engines(core, dst))

    def lands(src, sem, key):
        wr[key] = (sem, len(topo.engines(src, core)))

    def arr(name, k):
        return T["%s%d" % (name, k)]

    load("s", T.cui[:], T.cu[:], "dcu", "cui")
    load("y", T.Cx[:, 0:W], T.ck[:], "dck", "C")
    load("s", T.gapi[:], T.gap[:], "dgp", "gapi")
    load("y", T.Lt[:], T.la[:], "dla", "Lt")
    for t in (1, 2):
        lands(prv, "ae%d" % t, ("E", t))
        lands(prv, "an%d" % t, ("NU", t))
        for q in range(NQ):
            lands(prv, "al%d_%d" % (t, q), ("LI", t, q))
            lands(prv, "ab%d_%d" % (t, q), ("IB", t, q))
    lands(prv, "ag1", ("GP", 1))
    lands(pv2, "ag2", ("GP", 2))

    op("g", lambda: g.iota(T.j8[:], [[0, 16]], 0, 8), w=["j8"])
    op("g", lambda: g.iota(T.jq[:], [[128, 16]], 0, 0), w=["jq"])
    op("v", lambda: V.memset(T.ones[:], 1.0), w=["ones"])
    op("g", lambda: g.affine_select(T.tI[:], T.ones[:], [[-1, 128]], A.is_equal, 0.0, 0, 1), r=["ones"], w=["tI"])
    op("g", lambda: g.affine_select(T.tC[:], T.ones[:], [[-16, 8], [0, 16]], A.is_ge, 0.0, 0, 1), r=["ones"], w=["tC"])
    op("g", lambda: g.affine_select(T.tB[:], T.tC[:], [[16, 8], [0, 16]], A.is_ge, 0.0, 15, -1), r=["tC"], w=["tB"])
    op("g", lambda: g.iota(T.tj[:], [[0, 2], [-1, 128]], 128, 1), w=["tj"])
    for h in range(2):
        hs = slice(64 * h, 64 * h + 64)
        op("g", lambda: g.affine_select(T.tD[:, hs], T.ones[:, hs], [[0, 4], [-16, 16]], A.is_ge, 0.0, 128 * h, 1), r=["ones"], w=[("tD", h)])
        op("g", lambda: g.affine_select(T.tF[:, hs], T.tD[:, hs], [[0, 4], [16, 16]], A.is_ge, 0.0, 15 - 128 * h, -1), r=[("tD", h)], w=[("tF", h)])
    op("v", lambda: V.memset(T.mask[:], 1.0), w=["mask"])
    op("v", lambda: V.memset(T.mask[:, 0::16], 0.0), w=["mask"])
    op("v", lambda: V.memset(T.CSh[:], -2.5 / 16), w=["CSh"])
    op("v", lambda: V.tensor_scalar(T.j8a[:], T.j8[:], 127, None, A.bitwise_and), r=["j8"], w=["j8a"])
    op("v", lambda: V.tensor_tensor(T.i8[:], T.j8a[:], T.jq[:], A.add), r=["j8a", "jq"], w=["i8"])
    op("v", lambda: V.tensor_scalar(T.ic[:], T.i8[:], 3, None, A.logical_shift_right), r=["i8"], w=["ic"])
    op("v", lambda: V.tensor_scalar(T.E0[:, 0:16], T.ic[:], W, None, A.add), r=["ic"], w=[("E0", 4)])
    op("v", lambda: V.tensor_scalar(T.E1[:, 0:16], T.ic[:], W, None, A.add), r=["ic"], w=["E1d"])
    op("v", lambda: V.tensor_copy(T.IDh[:], T.tI[:]), r=["tI"], w=["IDh"])
    op("v", lambda: V.tensor_scalar(T.NKh[:], T.tI[:], -float(W), None, A.mult), r=["tI"], w=["NKh"])
    op("v", lambda: V.tensor_scalar(T.PKh[:], T.tI[:], float(W), None, A.mult), r=["tI"], w=["PKh"])
    op("v", lambda: V.tensor_scalar(T.BGh[:], T.tB[:], KB, None, A.mult), r=["tB"], w=["BGh"])
    op("v", lambda: V.tensor_scalar(T.NBh[:], T.tB[:], -KB, None, A.mult), r=["tB"], w=["NBh"])
    for k in range(4):
        op("v", lambda: V.tensor_scalar(T.cr[:, 16 * k:16 * k + 16], T.cui[:], k, None, A.add), r=["cui"], w=[("cr", k)])
    op("v", lambda: V.tensor_scalar(T.cm[:], T.cr[:], 7, None, A.bitwise_and), r=[("cr", k) for k in range(4)], w=["cm"])
    for k in range(4):
        op("v", lambda: V.tensor_tensor(T.E0[:, 16 + 16 * k:32 + 16 * k], T.cm[:, 16 * k:16 * k + 16], T.i8[:], A.add),
           r=["cm", "i8"], w=[("E0", k)])
    op("v", lambda: V.tensor_copy(T.ou[:], T.E0[:, 16:48]), r=[("E0", 0), ("E0", 1)], w=["ou"])
    op("v", lambda: V.tensor_copy(T.LI0[:], T.Cx[:, 0:W].indirect(T.ou[:, 0:16])), r=["C", "ou"],
       w=[("LI", 0, q) for q in range(NQ)])
    op("v", lambda: V.tensor_copy(T.I0[:], T.LI0[:]), r=[("LI", 0, q) for q in range(NQ)], w=[("IB", 0, q) for q in range(NQ)])
    op("v", lambda: V.tensor_copy(T.GP0[:], T.gapi[:]), r=["gapi"], w=[("GP", 0)])
    send(nxt, T.GP1[:], T.GP0[:], "ag1", [("GP", 0)])
    send(nx2, T.GP2[:], T.GP0[:], "ag2", [("GP", 0)])
    op("v", lambda: V.tensor_scalar(T.tk[:], T.tj[:], 15, None, A.bitwise_and), r=["tj"], w=["tk"])
    op("v", lambda: V.tensor_scalar(T.te[:], T.tk[:], 0, None, A.is_equal), r=["tk"], w=["te"])
    op("v", lambda: V.tensor_scalar(T.TH[:], T.te[:], -1048576.0, 1048576.0 + 2.5 * KB, A.mult, A.add), r=["te"], w=["TH"])
    op("v", lambda: V.tensor_scalar(T.Bh[:], T.tF[:], BIG, None, A.mult), r=[("tF", 0), ("tF", 1)], w=["Bh"])

    def cols(q):
        return slice(CH * q, CH * q + CH)

    def iap(t, q):
        return T.I0[:, cols(q)] if t == 0 else arr("IB", t)[:, 2 * CH * q:2 * CH * q + CH]

    def bap(t, q):
        return T.I0[:, cols(q)] if t == 0 else arr("IB", t)[:, 2 * CH * q + CH:2 * CH * q + 2 * CH]

    def a1(q):
        return T.AB[:, 256 + CH * q:256 + CH * q + CH]

    def Lg(t, q, b=0):
        k = HV * b
        op("s", lambda: S.activation(arr("X", q)[:, 16 * k:CW], T.Lt[:, 0:W].indirect(arr("LI", t)[:, CH * q + k:CH * q + CH]), COPY),
           r=["Lt", ("LI", t, q)], w=[("X", q, 1)] if b else [("X", q, 0), ("X", q, 1)])

    def Lv(t, q):
        op("v", lambda: V.tensor_copy(arr("X", q)[:, 0:16 * HV], T.Lt[:, 0:W].indirect(arr("LI", t)[:, CH * q:CH * q + HV])),
           r=["Lt", ("LI", t, q)], w=[("X", q, 0)])

    def Mx(t, q):
        op("v", lambda: V.tensor_tensor_scan(arr("R", q)[:], T.mask[:], arr("X", q)[:], 0.0, A.mult, A.max),
           r=["mask", ("X", q, 0), ("X", q, 1)], w=[("R", q)])

    def Ug(t, q, b):
        for k in range(8 * b, 8 * b + 8):
            o, key = arr("U", q % 2)[:, CH * k:CH * k + CH], ("U", q % 2, b)
            op("p", lambda: P.matmul(o, T.NKh[:], arr("X", q)[:, k::16], True, False), r=["NKh", ("X", q, 0), ("X", q, 1)], w=[key])
            op("p", lambda: P.matmul(o, T.PKh[:], arr("R", q)[:, 15::16], False, True), r=["PKh", ("R", q)], w=[key])

    def Wm(t, q, b):
        for k in range(8 * b, 8 * b + 8):
            op("v", lambda: V.tensor_tensor(arr("Wm", q)[:, k::16], arr("X", q)[:, k::16], arr("U", q % 2)[:, CH * k:CH * k + CH], A.min),
               r=[("X", q, 0), ("X", q, 1), ("U", q % 2, b)], w=[("Wm", q, k)])

    def Sc(t, q):
        op("v", lambda: V.tensor_tensor_scan(arr("S2", q)[:], T.mask[:], arr("Wm", q)[:], 0.0, A.mult, A.max),
           r=["mask"] + [("Wm", q, k) for k in range(16)], w=[("S2", q)])

    def Sk(t, q):
        op("v", lambda: V.tensor_copy(T.SL[:, cols(q)], arr("S2", q)[:, 15::16]), r=[("S2", q)], w=[("SL", q)])

    def Cg(t, q):
        k = TV if (t, q) == (ST - 1, NQ - 1) else 0
        op("s", lambda: S.activation(arr("Y", q)[:, 16 * k:CW], T.Cx[:, 0:W].indirect(T.SL[:, CH * q + k:CH * q + CH]), COPY),
           r=["C", ("SL", q)], w=[("Y", q)])

    def Cv(t, q):
        op("v", lambda: V.tensor_copy(arr("Y", q)[:, 0:16 * TV], T.Cx[:, 0:W].indirect(T.SL[:, CH * q:CH * q + TV])),
           r=["C", ("SL", q)], w=[("Yv", q)])

    def Rl(t):
        if t == 0:
            op("v", lambda: V.tensor_copy(T.REL[:], T.Cx[:, 0:W].indirect(T.ou[:, 16:32])), r=["C", "ou"], w=["REL"])
        else:
            op("s", lambda: S.activation(T.REL[:], T.Cx[:, 0:W].indirect(arr("NU", t)[:]), COPY), r=["C", ("NU", t)], w=["REL"])

    def PTI(t):
        for q in range(NQ):
            op("p", lambda: P.matmul(T.AB[:, cols(q)], T.IDh[:], iap(t, q), True, True), r=["IDh", ("IB", t, q)], w=["AB"])
        for q in range(NQ):
            op("p", lambda: P.matmul(T.TB[:, cols(q)], T.IDh[:], bap(t, q), True, False), r=["IDh", ("IB", t, q)], w=["TB"])
            op("p", lambda: P.matmul(T.TB[:, cols(q)], T.IDh[:], arr("GP", t)[:, cols(q)], False, True), r=[("GP", t)], w=["TB"])

    def Cm(t, q):
        op("v", lambda: V.tensor_tensor_scan(arr("R2", q)[:], T.mask[:], arr("Y", q)[:], 0.0, A.mult, A.max),
           r=["mask", ("Y", q), ("Yv", q)], w=[("R2", q)])

    def Ge(t, q):
        op("v", lambda: V.tensor_tensor(T.NEW[:, cols(q)], arr("R2", q)[:, 15::16], T.AB[:, cols(q)], A.max),
           r=[("R2", q), "AB"], w=[("NEW", q)])

    def Gb(t, q):
        op("v", lambda: V.tensor_tensor(T.GE[:, cols(q)], T.NEW[:, cols(q)], T.TB[:, cols(q)], A.is_ge),
           r=[("NEW", q), "TB"], w=[("GE", q)])

    def Pb(t, q):
        for k, m in ((0, "BGh"), (1, "NBh")):
            op("p", lambda: P.matmul(T.BK[:, CH * k:CH * k + CH], T[m][:], T.CSh[:, 0:CH], True, False), r=[m, "CSh"], w=["BK"])
            op("p", lambda: P.matmul(T.BK[:, CH * k:CH * k + CH], T[m][:], T.GE[:, cols(q)], False, True), r=[m, ("GE", q)], w=["BK"])

    def Se(t, q):
        op("v", lambda: V.tensor_tensor(a1(q), T.REL[:, cols(q)], T.BK[:, 0:CH], A.min), r=["REL", "BK", "AB"], w=[("a1", q)])
        op("v", lambda: V.tensor_tensor(T.A2[:, cols(q)], T.NEW[:, cols(q)], T.BK[:, CH:2 * CH], A.min), r=[("NEW", q), "BK"], w=[("A2", q)])

    def Sh(t, q):
        o = T.YO[:, cols(q)] if t == ST - 1 else arr("OB", t)[:, 2 * CH * q:2 * CH * q + CH]
        op("v", lambda: V.tensor_tensor(o, T.A2[:, cols(q)], a1(q), A.max), r=[("A2", q), ("a1", q), "AB"], w=[("OBi", t, q)])
        if t == ST - 1:
            send(nxt, T.YL[:, cols(q)], T.YO[:, cols(q)], "ay%d" % q, [("OBi", t, q)])

    def Sj(t, q):
        op("v", lambda: V.tensor_copy(arr("OL", t)[:, cols(q)], arr("OB", t)[:, 2 * CH * q:2 * CH * q + CH]), r=[("OBi", t, q)], w=[("OL", t, q)])
        send(nxt, arr("LI", t + 1)[:, cols(q)], arr("OL", t)[:, cols(q)], "al%d_%d" % (t + 1, q), [("OL", t, q)])

    def Sf(t, q):
        op("v", lambda: V.tensor_tensor(T.A3[:, cols(q)], bap(t, q), T.BK[:, CH:2 * CH], A.min), r=[("IB", t, q), "BK"], w=[("A3", q)])

    def Sb(t, q):
        ob = arr("OB", t)[:, 2 * CH * q + CH:2 * CH * q + 2 * CH]
        op("v", lambda: V.tensor_tensor(ob, T.A3[:, cols(q)], a1(q), A.max), r=[("A3", q), ("a1", q), "AB"], w=[("OBb", t, q)])
        send(nxt, arr("IB", t + 1)[:, 2 * CH * q:2 * CH * (q + 1)], arr("OB", t)[:, 2 * CH * q:2 * CH * (q + 1)], "ab%d_%d" % (t + 1, q),
             [("OBi", t, q), ("OBb", t, q)])

    def Pl(t):
        for h in range(2):
            op("p", lambda: P.matmul(T.TB[:, 256 + 128 * h:384 + 128 * h], T.GE[:, 128 * h:128 * h + 128], T.BGh[:], True, True),
               r=["BGh"] + [("GE", q) for q in range(NQ)], w=["TB"])

    def Vl(t):
        op("v", lambda: V.tensor_tensor(T.Ah[:], T.TB[:, 256:512], T.TH[:], A.is_ge), r=["TB", "TH"], w=["Ah"])

    def Pd(t):
        w = 16 * (4, 3, 1)[t]
        for h in range(2):
            op("p", lambda: P.matmul(T.BK[:, 128:128 + w], T.Ah[:, 128 * h:128 * h + 128], T.Bh[:, 64 * h:64 * h + w], h == 0, h == 1),
               r=["Ah", "Bh"], w=["BK"])

    def Sl(t):
        w = 16 * (4, 3, 1)[t]
        e = T.EC if t == ST - 1 else arr("E", t)
        src = [("E0", k) for k in range(5)] if t == 0 else [("E", t), "E1d"] if t == 1 else ["EC0", "EC1"]
        op("v", lambda: V.tensor_tensor(T.BK[:, 192:192 + w], e[:, 16:16 + w], T.BK[:, 128:128 + w], A.min), r=src + ["BK"], w=["lt1"])
        op("v", lambda: V.tensor_tensor(T.lt2[:, 0:w], e[:, 0:w], T.BK[:, 128:128 + w], A.subtract), r=src + ["BK"], w=["lt2"])

    def Sz(t):
        w = 16 * (4, 3, 1)[t]
        res = arr("RES", t)
        op("v", lambda: V.tensor_tensor(res[:, 0:w], T.lt2[:, 0:w], T.BK[:, 192:192 + w], A.max), r=["lt1", "lt2", "BK"], w=[("RES", t)])
        if t == ST - 1:
            send(nxt, T.YCL[:], res[:, 0:16], "ayc", [("RES", t)])

    def Sy(t):
        res = arr("RES", t)
        op("v", lambda: V.tensor_copy(arr("RU", t)[:], res[:, 0:48]), r=[("RES", t)], w=[("RU", t)])
        send(nxt, arr("NU", t + 1)[:], arr("RU", t)[:, 32:48], "an%d" % (t + 1), [("RU", t)])
        if t == 0:
            send(nxt, T.E1[:, 16:64], res[:, 16:64], "ae1", [("RES", t)])
        else:
            send(nxt, T.E2[:, 0:32], res[:, 16:48], "ae2", [("RES", t)])

    def Scat(t):
        op("v", lambda: V.tensor_copy(T.Cx[:, 0:W + NC].indirect(arr("RU", t)[:, 0:16]), T.NEW[:]),
           r=[("RU", t)] + [("NEW", q) for q in range(NQ)], w=["C"])

    def Ec(t):
        for k in range(2):
            op("v", lambda: V.tensor_tensor(T.EC[:, 16 * k:16 * k + 16], T.E2[:, 16 * k:16 * k + 16], T.i8[:], A.subtract),
               r=[("E", 2), "i8"], w=["EC%d" % k])

    parts = {"L": Lg, "l": Lv, "M": Mx, "U": Ug, "W": Wm, "S": Sc, "k": Sk, "C": Cg, "c": Cv, "R": Rl, "P": PTI, "m": Cm, "G": Ge, "g": Gb,
             "B": Pb, "E": Se, "H": Sh, "J": Sj, "F": Sf, "K": Sb, "p": Pl, "v": Vl, "d": Pd, "s": Sl, "z": Sz, "y": Sy, "x": Scat, "e": Ec}
    for tok in SCHED.split():
        parts[tok[0]](*[int(c) for c in tok[1:]])

    for q in range(NQ):
        wait("y", "ay%d" % q, len(topo.engines(prv, core)))
        g.sync.dma_start(T.yi[:, cols(q)], T.YL[:, cols(q)]).then_inc(T.sem.dout, 16)
    wait("s", "ayc", len(topo.engines(prv, core)))
    S.dma_start(T.yc[:], T.YCL[:]).then_inc(T.sem.dyc, 16)
    wait("s", "dyc", 16)
    wait("y", "dout", 16 * NQ)
    for q in own:
        wait("g", own[q], cnt[q])
    wait("g", "loc", tot["loc"])
